import numpy as np
import ml_dtypes


def mxq(x, axis, fmt="e4m3"):
    dtype, down = {"e4m3": (ml_dtypes.float8_e4m3fn, 7), "e5m2": (ml_dtypes.float8_e5m2, 14)}[fmt]
    v = np.moveaxis(np.asarray(x, np.float32).astype(ml_dtypes.bfloat16).astype(np.float64), axis, -1)
    blocks = v.reshape(v.shape[:-1] + (-1, 32))
    amax = np.abs(blocks).max(-1, keepdims=True)
    byte = np.maximum(np.where(amax > 0, np.frexp(amax)[1] - 1 + 127, 0) - down, 1)
    scale = np.exp2(byte - 127.0)
    codes = (blocks / scale).astype(np.float32).astype(dtype).astype(np.float64)
    return np.moveaxis((codes * scale).reshape(v.shape), -1, axis)


WIDE = False


def mx_kscale(k):
    if not WIDE:
        return np.ones(k)
    levels = np.array([10, -10, 5, -5, 0])
    if k % 512:
        return np.exp2(np.random.permutation(np.resize(levels, k // 32))).repeat(32)
    a = np.empty((k // 512, 16))
    for p in range(k // 512):
        a[p, :8] = np.random.permutation(np.resize(levels, 8))
        for g in range(8):
            far = levels[np.abs(levels - a[p, g]) >= 10]
            a[p, g + 8] = far[np.random.randint(len(far))]
    return np.exp2(a.ravel()).repeat(32)


BF16 = ml_dtypes.bfloat16


def bf(x):
    return np.asarray(x, np.float32).astype(BF16)


def f64(x):
    return np.asarray(x).astype(np.float64)


M, K, F, N = 2048, 1024, 1024, 1024


def draw0():
    s = mx_kscale(K)
    u = mx_kscale(M)
    x = np.random.standard_normal((M, K)) * s
    c = np.random.standard_normal((K, F)) / np.sqrt(K) / s[:, None]
    offset = 0.4 * np.random.standard_normal(F)
    gain = -(1.0 + 0.3 * np.random.standard_normal(M)) * u
    bmat = np.random.standard_normal((N, M)) / np.sqrt(M) / u
    return {"x": bf(x),
            "c": bf(c),
            "offset": bf(offset),
            "gain": bf(gain),
            "bmat": bf(bmat)}


def core(x, c, offset, gain, bmat):
    sigma = mxq(f64(x), 1, "e4m3") @ mxq(f64(c), 0, "e4m3")
    ctrl = f64(gain)[:, None] * np.tanh(sigma + f64(offset))
    v = mxq(f64(bmat), 1, "e4m3") @ mxq(ctrl, 0, "e4m3")
    return v


def e4m3fn_bytes(y):
    return np.clip(np.asarray(y, np.float64), -448.0, 448.0).astype(np.float32).astype(ml_dtypes.float8_e4m3fn).view(np.uint8)


def e4m3fn_values(b):
    return np.asarray(b, np.uint8).view(ml_dtypes.float8_e4m3fn).astype(np.float64)


def setup_inputs():
    d = draw0()
    x0 = np.asarray(d['x']).astype(np.float64)
    s = (np.max(np.abs(x0), axis=(0,), keepdims=True) / 448.0).astype(np.float32)
    out = {}
    for k, v in d.items():
        if k == 'x':
            out['x_bytes'] = e4m3fn_bytes(x0 / s.astype(np.float64))
            out['x_scale'] = s
        else:
            out[k] = v
    return out


def reference(x_bytes, x_scale, c, offset, gain, bmat):
    return core(e4m3fn_values(x_bytes) * x_scale.astype(np.float64), c, offset, gain, bmat)

@@ -1,0 +1,317 @@
+from contextlib import ExitStack
+
+import concourse.mybir as mybir
+from concourse.masks import make_identity
+
+M, K, F, N = 2048, 1024, 1024, 1024
+FLOPS = 2 * M * K * F + 2 * N * M * F
+
+F32 = mybir.dt.float32
+BF16 = mybir.dt.bfloat16
+U32 = mybir.dt.uint32
+U8 = mybir.dt.uint8
+FP8 = mybir.dt.float8_e4m3fn
+FP8X4 = mybir.dt.float8_e4m3fn_x4
+ACT = mybir.ActivationFunctionType
+MULT = mybir.AluOpType.mult
+
+P = 128
+G = M // 512
+Q = K // 512
+FT = F // P
+NT = N // P
+CH = 4
+FC = F // CH
+FPC = FC // P
+
+
+def tile_networked_sliding_control_s7_kernel(tc, x_bytes, x_scale, c, offset, gain, bmat, out):
+    nc = tc.nc
+    with ExitStack() as ctx:
+        const = ctx.enter_context(tc.tile_pool(name="const", bufs=1))
+        pool = ctx.enter_context(tc.tile_pool(name="work", bufs=2))
+        psum = ctx.enter_context(tc.psum_pool(name="psum", bufs=4))
+
+        x_view = x_bytes.rearrange("(g p t) k -> g p t k", p=P, t=4)
+        c_view = c.rearrange("(q p j) (h f) -> q h p j f", p=P, j=4, h=2)
+        b_view = bmat.rearrange("(n p) m -> n p m", p=P)
+        x_raw, c_raw, b_raw = {}, {}, {}
+
+        def load_x(g, parts=1):
+            xbytes = pool.tile([P, 4, K], U8, bufs=3, name="xbytes")
+            step = 4 // parts
+            x_raw[g] = xbytes
+            return [lambda i=i: nc.sync.dma_start(out=xbytes[:, i * step : (i + 1) * step, :], in_=x_view[g][:, i * step : (i + 1) * step, :]) for i in range(parts)]
+
+        def load_c(q, h):
+            raw = pool.tile([P, 4, 512], BF16, bufs=7, name="raw")
+            nc.sync.dma_start(out=raw[:], in_=c_view[q, h])
+            c_raw[q, h] = raw
+
+        def load_b(n):
+            raw = pool.tile([P, 4, 512], BF16, bufs=7, name="raw")
+            nc.sync.dma_start(out=raw[:].rearrange("p a b -> p (a b)"), in_=b_view[n])
+            b_raw[n] = raw
+
+        c_int, c_codes, x_codes, b_codes, k_codes = {}, {}, {}, {}, {}
+        x_wide, x_tp, x_int, b_tp, b_int = {}, {}, {}, {}, {}
+
+        def c_inter(q, h, eng):
+            cint = pool.tile([P, 512, 4], BF16, bufs=2, name="cint", align_bytes=64)
+            dst = cint[:].rearrange("p (c i) t -> p c t i", i=4)
+            src = c_raw[q, h][:].rearrange("p t (c i) -> p c t i", i=4)
+            if eng == "v":
+                nc.vector.tensor_copy(out=dst, in_=src)
+            else:
+                nc.scalar.copy(out=dst, in_=src)
+            c_int[q, h] = cint
+
+        def c_quant(q, h):
+            codes = const.tile([P, 512], U32, name=f"cc{q}{h}", align_bytes=64)
+            scales = const.tile([P, 512], U8, name=f"cs{q}{h}", align_bytes=64)
+            nc.vector.quantize_mx(out=codes[:].bitcast(FP8X4), scales=scales[:], in_=c_int[q, h][:].rearrange("p f t -> p (f t)"))
+            c_codes[q, h] = (codes, scales)
+
+        def widen(g, t):
+            xw = pool.tile([P, K], BF16, bufs=3, name="xw")
+            nc.vector.tensor_tensor(out=xw[:], in0=x_raw[g][:, t, :].bitcast(FP8), in1=scale_b[:], op=MULT)
+            x_wide[g, t] = xw
+
+        def x_turn(g, t):
+            words = x_wide[g, t][:].bitcast(F32)
+            tp = psum.tile([P, 4, P], F32, name="tp")
+            for q in range(Q):
+                for u in range(2):
+                    nc.tensor.transpose(tp[:, 2 * q + u, :], words[:, 256 * q + u : 256 * (q + 1) : 2], ident[:])
+            x_tp[g, t] = tp
+
+        def x_copy(g, t):
+            if t == 0:
+                xint = pool.tile([P, Q, 512, 4], BF16, bufs=2, name="xint", align_bytes=64)
+                x_int[g] = xint
+            view = x_int[g][:].rearrange("p q r j -> p (q r j)").bitcast(F32).rearrange("p (q r u) -> p q r u", q=Q, u=2)
+            nc.scalar.copy(out=view[:, :, t * P : (t + 1) * P, :], in_=x_tp[g, t][:].rearrange("p (q u) r -> p q r u", u=2))
+
+        def x_quant(g):
+            codes = const.tile([P, Q, 512], U32, name=f"xc{g}", align_bytes=64)
+            scales = const.tile([P, Q, 512], U8, name=f"xs{g}", align_bytes=64)
+            nc.vector.quantize_mx(
+                out=codes[:].rearrange("p q r -> p (q r)").bitcast(FP8X4),
+                scales=scales[:].rearrange("p q r -> p (q r)"),
+                in_=x_int[g][:].rearrange("p q r j -> p (q r j)"),
+            )
+            x_codes[g] = (codes, scales)
+
+        def b_turn(n, half):
+            words = b_raw[n][:].rearrange("p a b -> p (a b)").bitcast(F32)
+            tp = psum.tile([P, 4, P], F32, name="tp")
+            for gl in range(2):
+                g = 2 * half + gl
+                for u in range(2):
+                    nc.tensor.transpose(tp[:, 2 * gl + u, :], words[:, 256 * g + u : 256 * (g + 1) : 2], ident[:])
+            b_tp[n, half] = tp
+
+        def b_copy(n, half, eng):
+            if half == 0:
+                bint = pool.tile([P, G, P, 4], BF16, bufs=2, name="bint", align_bytes=64)
+                b_int[n] = bint
+            view = b_int[n][:].rearrange("p g r j -> p (g r j)").bitcast(F32).rearrange("p (g r u) -> p g r u", g=G, u=2)
+            dst = view[:, 2 * half : 2 * half + 2, :, :]
+            src = b_tp[n, half][:].rearrange("p (g u) r -> p g r u", u=2)
+            if eng == "v":
+                nc.vector.tensor_copy(out=dst, in_=src)
+            else:
+                nc.scalar.copy(out=dst, in_=src)
+
+        def b_quant(n):
+            codes = const.tile([P, G, P], U32, name=f"bc{n}", align_bytes=64)
+            scales = const.tile([P, G, P], U8, name=f"bs{n}", align_bytes=64)
+            nc.vector.quantize_mx(
+                out=codes[:].rearrange("p g r -> p (g r)").bitcast(FP8X4),
+                scales=scales[:].rearrange("p g r -> p (g r)"),
+                in_=b_int[n][:].rearrange("p g r j -> p (g r j)"),
+            )
+            b_codes[n] = (codes, scales)
+
+        s_ps, tanh_t, k_wide, k_tp, k_int = {}, {}, {}, {}, {}
+
+        def sigma(g, ft):
+            ps = psum.tile([P, 512], F32, name="mm")
+            h, col = ft // 4, slice((ft % 4) * P, (ft % 4 + 1) * P)
+            xc, xs = x_codes[g]
+            for q in range(Q):
+                cc, cs = c_codes[q, h]
+                nc.tensor.matmul_mx(
+                    out=ps[:],
+                    lhsT=cc[:, col].bitcast(FP8X4),
+                    lhsT_scale=cs[:, col],
+                    rhs=xc[:, q, :].bitcast(FP8X4),
+                    rhs_scale=xs[:, q, :],
+                    start=(q == 0),
+                    stop=(q == Q - 1),
+                )
+            s_ps[g, ft] = ps
+
+        def tanh(g, ft):
+            th = pool.tile([P, 512], F32, bufs=28, name="th")
+            nc.scalar.activation(out=th[:], in_=s_ps[g, ft][:], func=ACT.Tanh, bias=off_cols[:, ft : ft + 1])
+            tanh_t[g, ft] = th
+
+        def k_gain(g, ft):
+            kw = pool.tile([P, 512], BF16, bufs=6, name="kw")
+            nc.vector.tensor_tensor(
+                out=kw[:].rearrange("f (u p e) -> f u p e", u=2, e=2),
+                in0=tanh_t[g, ft][:].rearrange("f (u e p) -> f u p e", u=2, e=2),
+                in1=gain_b[:, 512 * g : 512 * (g + 1)].rearrange("f (p u e) -> f u p e", u=2, e=2),
+                op=MULT,
+            )
+            k_wide[g, ft] = kw
+
+        def k_turn(g, ch):
+            tp = psum.tile([P, 4, P], F32, name="tp")
+            for i in range(FPC):
+                words = k_wide[g, ch * FPC + i][:].bitcast(F32)
+                for u in range(2):
+                    nc.tensor.transpose(tp[:, 2 * i + u, :], words[:, P * u : P * (u + 1)], ident[:])
+            k_tp[g, ch] = tp
+
+        def k_copy(g, ch):
+            kint = pool.tile([P, FPC, P, 4], BF16, bufs=3, name="kint", align_bytes=64)
+            view = kint[:].rearrange("p i f j -> p (i f j)").bitcast(F32).rearrange("p (i f u) -> p i f u", i=FPC, u=2)
+            nc.scalar.copy(out=view, in_=k_tp[g, ch][:].rearrange("p (i u) f -> p i f u", u=2))
+            k_int[g, ch] = kint
+
+        def k_quant(g, ch):
+            codes = const.tile([P, FC], U32, name=f"kc{g}_{ch}", align_bytes=64)
+            scales = const.tile([P, FC], U8, name=f"ks{g}_{ch}", align_bytes=64)
+            nc.vector.quantize_mx(out=codes[:].bitcast(FP8X4), scales=scales[:], in_=k_int[g, ch][:].rearrange("p i f j -> p (i f j)"))
+            k_codes[g, ch] = (codes, scales)
+
+        def second(ch, pair, eng):
+            ps = psum.tile([P, 2, FC], F32, name="mm")
+            for i in range(2):
+                bc, bs = b_codes[2 * pair + i]
+                for g in range(G):
+                    kc, ks = k_codes[g, ch]
+                    nc.tensor.matmul_mx(
+                        out=ps[:, i, :],
+                        lhsT=bc[:, g, :].bitcast(FP8X4),
+                        lhsT_scale=bs[:, g, :],
+                        rhs=kc[:].bitcast(FP8X4),
+                        rhs_scale=ks[:],
+                        start=(g == 0),
+                        stop=(g == G - 1),
+                    )
+            vo = pool.tile([P, 2, FC], F32, bufs=3, name="vo")
+            if eng == "s":
+                nc.scalar.copy(out=vo[:], in_=ps[:])
+            else:
+                nc.vector.tensor_copy(out=vo[:], in_=ps[:])
+            nc.sync.dma_start(
+                out=out[2 * pair * P : 2 * (pair + 1) * P, ch * FC : (ch + 1) * FC].rearrange("(i p) f -> p i f", i=2),
+                in_=vo[:],
+            )
+
+        ident = const.tile([P, P], F32)
+        make_identity(nc, ident[:])
+        off_rows = const.tile([P, P], BF16)
+        nc.gpsimd.memset(off_rows[:], 0.0)
+        warm = const.tile([P, 1], F32)
+        nc.gpsimd.memset(warm[:], 0.0)
+        warm_out = const.tile([P, 1], F32)
+        scale_b = const.tile([P, K], F32)
+        gain_b = const.tile([P, M], BF16)
+        scale_v = const.tile([P, 8], F32)
+        off_f = const.tile([P, P], F32)
+        off_cols = const.tile([P, FT], F32)
+
+        nc.scalar.dma_start(out=scale_v[:], in_=x_scale.rearrange("o (p m) -> (o p) m", m=8))
+        nc.scalar.activation(out=warm_out[:], in_=warm[:], func=ACT.Tanh)
+        x0 = load_x(0, 2)
+        x0[0]()
+        x0[1]()
+        load_c(0, 0)
+        load_c(1, 0)
+        load_b(0)
+        nc.scalar.dma_start(out=off_rows[0:FT, :], in_=offset.rearrange("(c p) -> c p", p=P))
+        load_b(1)
+        load_b(2)
+        load_b(3)
+        load_b(4)
+        load_x(1)[0]()
+        load_c(0, 1)
+        load_c(1, 1)
+        load_x(2)[0]()
+        load_b(5)
+        load_b(6)
+        load_b(7)
+        nc.scalar.dma_start(out=gain_b[:], in_=gain.partition_broadcast(P))
+        for half in range(2):
+            sp = psum.tile([P, 4, P], F32, name="tp")
+            for i in range(4):
+                nc.tensor.transpose(sp[:, i, :], scale_v[:, 4 * half + i : 4 * half + i + 1].to_broadcast([P, P]), ident[:])
+            dst = scale_b[:].rearrange("p (n m) -> p n m", m=8)[:, :, 4 * half : 4 * half + 4]
+            if half:
+                nc.vector.tensor_copy(out=dst, in_=sp[:].rearrange("p m n -> p n m"))
+            else:
+                nc.scalar.copy(out=dst, in_=sp[:].rearrange("p m n -> p n m"))
+
+        def prep_x(g):
+            for t in range(4):
+                widen(g, t)
+                x_turn(g, t)
+                x_copy(g, t)
+            x_quant(g)
+
+        def prep_b(n, e0="s", e1="s"):
+            for half in range(2):
+                b_turn(n, half)
+                b_copy(n, half, e1 if half else e0)
+            b_quant(n)
+
+        def ctrl(g, ch):
+            for i in range(FPC):
+                k_gain(g, ch * FPC + i)
+            k_turn(g, ch)
+            k_copy(g, ch)
+            k_quant(g, ch)
+
+        def off_prep():
+            nc.scalar.copy(out=off_f[:], in_=off_rows[:])
+            off_ps = psum.tile([P, 4, P], F32, name="tp")
+            nc.tensor.transpose(off_ps[:, 0, :], off_f[:], ident[:])
+            nc.scalar.copy(out=off_cols[:], in_=off_ps[:, 0, 0:FT])
+
+        prep_b(0, "s", "v")
+        c_inter(0, 0, "v")
+        for t in range(4):
+            widen(0, t); x_turn(0, t); x_copy(0, t)
+        c_inter(1, 0, "s")
+        c_quant(0, 0)
+        x_quant(0)
+        c_quant(1, 0)
+        off_prep()
+        prep_b(1, "s", "s")
+        prep_b(2, "s", "s")
+        c_inter(0, 1, "v")
+        c_inter(1, 1, "s")
+        c_quant(0, 1)
+        c_quant(1, 1)
+        for g in range(G):
+            for ft in range(FT):
+                sigma(g, ft)
+                tanh(g, ft)
+            if g + 1 < G:
+                prep_x(g + 1)
+            ctrl(g, 0)
+            if g == 0:
+                load_x(3)[0]()
+            for n in {0: (3, 4), 1: (5, 6), 2: (7,), 3: ()}[g]:
+                prep_b(n, "s", "s")
+        for ch in range(1, CH):
+            for g in range(G):
+                ctrl(g, ch)
+            for pair in range(NT // 2):
+                second(ch - 1, pair, "s")
+        for pair in range(NT // 2):
+            second(CH - 1, pair, "s" if pair % 2 else "v")

@@ -23,6 +23,8 @@ NT = N // P
 CH = 4
 FC = F // CH
 FPC = FC // P
+BANKS = 8
+BUFS = {"braw": 6, "cint": 2, "xw": 4, "xint": 2, "bint": 8, "thmod": 4, "kw": 8, "kint": 4, "xb": 4}
 
 
 def tile_networked_sliding_control_s7_kernel(tc, x_bytes, x_scale, c, offset, gain, bmat, out):
@@ -30,194 +32,49 @@ def tile_networked_sliding_control_s7_kernel(tc, x_bytes, x_scale, c, offset, ga
     with ExitStack() as ctx:
         const = ctx.enter_context(tc.tile_pool(name="const", bufs=1))
         pool = ctx.enter_context(tc.tile_pool(name="work", bufs=2))
-        psum = ctx.enter_context(tc.psum_pool(name="psum", bufs=4))
+        psum = ctx.enter_context(tc.psum_pool(name="psum", bufs=1))
 
-        x_view = x_bytes.rearrange("(g p t) k -> g p t k", p=P, t=4)
+        x_view = x_bytes.rearrange("(g p u e) k -> g u p e k", p=P, u=2, e=2)
         c_view = c.rearrange("(q p j) (h f) -> q h p j f", p=P, j=4, h=2)
         b_view = bmat.rearrange("(n p) m -> n p m", p=P)
         x_raw, c_raw, b_raw = {}, {}, {}
+        banks_taken = []
 
-        def load_x(g, parts=1):
-            xbytes = pool.tile([P, 4, K], U8, bufs=3, name="xbytes")
-            step = 4 // parts
-            x_raw[g] = xbytes
-            return [lambda i=i: nc.sync.dma_start(out=xbytes[:, i * step : (i + 1) * step, :], in_=x_view[g][:, i * step : (i + 1) * step, :]) for i in range(parts)]
+        def bank():
+            tile = psum.tile([P, 512], F32, name=f"bank{len(banks_taken) % BANKS}")
+            banks_taken.append(tile)
+            return tile
+
+        def copy(eng, dst, src):
+            if eng == "v":
+                nc.vector.tensor_copy(out=dst, in_=src)
+            else:
+                nc.scalar.copy(out=dst, in_=src)
+
+        def quantise(name, src, width):
+            codes = const.tile([P, width], U32, name=f"codes_{name}", align_bytes=256)
+            scales = const.tile([P, width], U8, name=f"scales_{name}", align_bytes=256)
+            nc.vector.quantize_mx(out=codes[:].bitcast(FP8X4), scales=scales[:], in_=src)
+            return codes, scales
+
+        def load_x(g, u):
+            xbytes = pool.tile([P, 2, K], U8, bufs=BUFS["xb"], name="xbytes")
+            nc.sync.dma_start(out=xbytes[:], in_=x_view[g, u])
+            x_raw[g, u] = xbytes
 
         def load_c(q, h):
-            raw = pool.tile([P, 4, 512], BF16, bufs=7, name="raw")
+            raw = pool.tile([P, 4, 512], BF16, bufs=BUFS["braw"], name="raw")
             nc.sync.dma_start(out=raw[:], in_=c_view[q, h])
             c_raw[q, h] = raw
 
         def load_b(n):
-            raw = pool.tile([P, 4, 512], BF16, bufs=7, name="raw")
-            nc.sync.dma_start(out=raw[:].rearrange("p a b -> p (a b)"), in_=b_view[n])
+            raw = pool.tile([P, M], BF16, bufs=BUFS["braw"], name="raw")
+            nc.sync.dma_start(out=raw[:], in_=b_view[n])
             b_raw[n] = raw
 
-        c_int, c_codes, x_codes, b_codes, k_codes = {}, {}, {}, {}, {}
-        x_wide, x_tp, x_int, b_tp, b_int = {}, {}, {}, {}, {}
-
-        def c_inter(q, h, eng):
-            cint = pool.tile([P, 512, 4], BF16, bufs=2, name="cint", align_bytes=64)
-            dst = cint[:].rearrange("p (c i) t -> p c t i", i=4)
-            src = c_raw[q, h][:].rearrange("p t (c i) -> p c t i", i=4)
-            if eng == "v":
-                nc.vector.tensor_copy(out=dst, in_=src)
-            else:
-                nc.scalar.copy(out=dst, in_=src)
-            c_int[q, h] = cint
-
-        def c_quant(q, h):
-            codes = const.tile([P, 512], U32, name=f"cc{q}{h}", align_bytes=64)
-            scales = const.tile([P, 512], U8, name=f"cs{q}{h}", align_bytes=64)
-            nc.vector.quantize_mx(out=codes[:].bitcast(FP8X4), scales=scales[:], in_=c_int[q, h][:].rearrange("p f t -> p (f t)"))
-            c_codes[q, h] = (codes, scales)
-
-        def widen(g, t):
-            xw = pool.tile([P, K], BF16, bufs=3, name="xw")
-            nc.vector.tensor_tensor(out=xw[:], in0=x_raw[g][:, t, :].bitcast(FP8), in1=scale_b[:], op=MULT)
-            x_wide[g, t] = xw
-
-        def x_turn(g, t):
-            words = x_wide[g, t][:].bitcast(F32)
-            tp = psum.tile([P, 4, P], F32, name="tp")
-            for q in range(Q):
-                for u in range(2):
-                    nc.tensor.transpose(tp[:, 2 * q + u, :], words[:, 256 * q + u : 256 * (q + 1) : 2], ident[:])
-            x_tp[g, t] = tp
-
-        def x_copy(g, t):
-            if t == 0:
-                xint = pool.tile([P, Q, 512, 4], BF16, bufs=2, name="xint", align_bytes=64)
-                x_int[g] = xint
-            view = x_int[g][:].rearrange("p q r j -> p (q r j)").bitcast(F32).rearrange("p (q r u) -> p q r u", q=Q, u=2)
-            nc.scalar.copy(out=view[:, :, t * P : (t + 1) * P, :], in_=x_tp[g, t][:].rearrange("p (q u) r -> p q r u", u=2))
-
-        def x_quant(g):
-            codes = const.tile([P, Q, 512], U32, name=f"xc{g}", align_bytes=64)
-            scales = const.tile([P, Q, 512], U8, name=f"xs{g}", align_bytes=64)
-            nc.vector.quantize_mx(
-                out=codes[:].rearrange("p q r -> p (q r)").bitcast(FP8X4),
-                scales=scales[:].rearrange("p q r -> p (q r)"),
-                in_=x_int[g][:].rearrange("p q r j -> p (q r j)"),
-            )
-            x_codes[g] = (codes, scales)
-
-        def b_turn(n, half):
-            words = b_raw[n][:].rearrange("p a b -> p (a b)").bitcast(F32)
-            tp = psum.tile([P, 4, P], F32, name="tp")
-            for gl in range(2):
-                g = 2 * half + gl
-                for u in range(2):
-                    nc.tensor.transpose(tp[:, 2 * gl + u, :], words[:, 256 * g + u : 256 * (g + 1) : 2], ident[:])
-            b_tp[n, half] = tp
-
-        def b_copy(n, half, eng):
-            if half == 0:
-                bint = pool.tile([P, G, P, 4], BF16, bufs=2, name="bint", align_bytes=64)
-                b_int[n] = bint
-            view = b_int[n][:].rearrange("p g r j -> p (g r j)").bitcast(F32).rearrange("p (g r u) -> p g r u", g=G, u=2)
-            dst = view[:, 2 * half : 2 * half + 2, :, :]
-            src = b_tp[n, half][:].rearrange("p (g u) r -> p g r u", u=2)
-            if eng == "v":
-                nc.vector.tensor_copy(out=dst, in_=src)
-            else:
-                nc.scalar.copy(out=dst, in_=src)
-
-        def b_quant(n):
-            codes = const.tile([P, G, P], U32, name=f"bc{n}", align_bytes=64)
-            scales = const.tile([P, G, P], U8, name=f"bs{n}", align_bytes=64)
-            nc.vector.quantize_mx(
-                out=codes[:].rearrange("p g r -> p (g r)").bitcast(FP8X4),
-                scales=scales[:].rearrange("p g r -> p (g r)"),
-                in_=b_int[n][:].rearrange("p g r j -> p (g r j)"),
-            )
-            b_codes[n] = (codes, scales)
-
-        s_ps, tanh_t, k_wide, k_tp, k_int = {}, {}, {}, {}, {}
-
-        def sigma(g, ft):
-            ps = psum.tile([P, 512], F32, name="mm")
-            h, col = ft // 4, slice((ft % 4) * P, (ft % 4 + 1) * P)
-            xc, xs = x_codes[g]
-            for q in range(Q):
-                cc, cs = c_codes[q, h]
-                nc.tensor.matmul_mx(
-                    out=ps[:],
-                    lhsT=cc[:, col].bitcast(FP8X4),
-                    lhsT_scale=cs[:, col],
-                    rhs=xc[:, q, :].bitcast(FP8X4),
-                    rhs_scale=xs[:, q, :],
-                    start=(q == 0),
-                    stop=(q == Q - 1),
-                )
-            s_ps[g, ft] = ps
-
-        def tanh(g, ft):
-            th = pool.tile([P, 512], F32, bufs=28, name="th")
-            nc.scalar.activation(out=th[:], in_=s_ps[g, ft][:], func=ACT.Tanh, bias=off_cols[:, ft : ft + 1])
-            tanh_t[g, ft] = th
-
-        def k_gain(g, ft):
-            kw = pool.tile([P, 512], BF16, bufs=6, name="kw")
-            nc.vector.tensor_tensor(
-                out=kw[:].rearrange("f (u p e) -> f u p e", u=2, e=2),
-                in0=tanh_t[g, ft][:].rearrange("f (u e p) -> f u p e", u=2, e=2),
-                in1=gain_b[:, 512 * g : 512 * (g + 1)].rearrange("f (p u e) -> f u p e", u=2, e=2),
-                op=MULT,
-            )
-            k_wide[g, ft] = kw
-
-        def k_turn(g, ch):
-            tp = psum.tile([P, 4, P], F32, name="tp")
-            for i in range(FPC):
-                words = k_wide[g, ch * FPC + i][:].bitcast(F32)
-                for u in range(2):
-                    nc.tensor.transpose(tp[:, 2 * i + u, :], words[:, P * u : P * (u + 1)], ident[:])
-            k_tp[g, ch] = tp
-
-        def k_copy(g, ch):
-            kint = pool.tile([P, FPC, P, 4], BF16, bufs=3, name="kint", align_bytes=64)
-            view = kint[:].rearrange("p i f j -> p (i f j)").bitcast(F32).rearrange("p (i f u) -> p i f u", i=FPC, u=2)
-            nc.scalar.copy(out=view, in_=k_tp[g, ch][:].rearrange("p (i u) f -> p i f u", u=2))
-            k_int[g, ch] = kint
-
-        def k_quant(g, ch):
-            codes = const.tile([P, FC], U32, name=f"kc{g}_{ch}", align_bytes=64)
-            scales = const.tile([P, FC], U8, name=f"ks{g}_{ch}", align_bytes=64)
-            nc.vector.quantize_mx(out=codes[:].bitcast(FP8X4), scales=scales[:], in_=k_int[g, ch][:].rearrange("p i f j -> p (i f j)"))
-            k_codes[g, ch] = (codes, scales)
-
-        def second(ch, pair, eng):
-            ps = psum.tile([P, 2, FC], F32, name="mm")
-            for i in range(2):
-                bc, bs = b_codes[2 * pair + i]
-                for g in range(G):
-                    kc, ks = k_codes[g, ch]
-                    nc.tensor.matmul_mx(
-                        out=ps[:, i, :],
-                        lhsT=bc[:, g, :].bitcast(FP8X4),
-                        lhsT_scale=bs[:, g, :],
-                        rhs=kc[:].bitcast(FP8X4),
-                        rhs_scale=ks[:],
-                        start=(g == 0),
-                        stop=(g == G - 1),
-                    )
-            vo = pool.tile([P, 2, FC], F32, bufs=3, name="vo")
-            if eng == "s":
-                nc.scalar.copy(out=vo[:], in_=ps[:])
-            else:
-                nc.vector.tensor_copy(out=vo[:], in_=ps[:])
-            nc.sync.dma_start(
-                out=out[2 * pair * P : 2 * (pair + 1) * P, ch * FC : (ch + 1) * FC].rearrange("(i p) f -> p i f", i=2),
-                in_=vo[:],
-            )
-
         ident = const.tile([P, P], F32)
-        make_identity(nc, ident[:])
         off_rows = const.tile([P, P], BF16)
-        nc.gpsimd.memset(off_rows[:], 0.0)
         warm = const.tile([P, 1], F32)
-        nc.gpsimd.memset(warm[:], 0.0)
         warm_out = const.tile([P, 1], F32)
         scale_b = const.tile([P, K], F32)
         gain_b = const.tile([P, M], BF16)
@@ -225,93 +82,323 @@ def tile_networked_sliding_control_s7_kernel(tc, x_bytes, x_scale, c, offset, ga
         off_f = const.tile([P, P], F32)
         off_cols = const.tile([P, FT], F32)
 
-        nc.scalar.dma_start(out=scale_v[:], in_=x_scale.rearrange("o (p m) -> (o p) m", m=8))
-        nc.scalar.activation(out=warm_out[:], in_=warm[:], func=ACT.Tanh)
-        x0 = load_x(0, 2)
-        x0[0]()
-        x0[1]()
-        load_c(0, 0)
-        load_c(1, 0)
-        load_b(0)
-        nc.scalar.dma_start(out=off_rows[0:FT, :], in_=offset.rearrange("(c p) -> c p", p=P))
-        load_b(1)
-        load_b(2)
-        load_b(3)
-        load_b(4)
-        load_x(1)[0]()
-        load_c(0, 1)
-        load_c(1, 1)
-        load_x(2)[0]()
-        load_b(5)
-        load_b(6)
-        load_b(7)
-        nc.scalar.dma_start(out=gain_b[:], in_=gain.partition_broadcast(P))
-        for half in range(2):
-            sp = psum.tile([P, 4, P], F32, name="tp")
+        def load_scale():
+            nc.scalar.dma_start(out=scale_v[:], in_=x_scale.rearrange("o (p m) -> (o p) m", m=8))
+
+        def load_offset():
+            nc.scalar.dma_start(out=off_rows[0:FT, :], in_=offset.rearrange("(c p) -> c p", p=P))
+
+        def load_gain():
+            nc.sync.dma_start(out=gain_b[:], in_=gain.partition_broadcast(P))
+
+        def warm_tanh():
+            nc.scalar.activation(out=warm_out[:], in_=warm[:], func=ACT.Tanh)
+
+        def spread_scale(half, eng):
+            sp = bank()
             for i in range(4):
-                nc.tensor.transpose(sp[:, i, :], scale_v[:, 4 * half + i : 4 * half + i + 1].to_broadcast([P, P]), ident[:])
+                col = 4 * half + i
+                nc.tensor.transpose(sp[:, i * P : (i + 1) * P], scale_v[:, col : col + 1].to_broadcast([P, P]), ident[:])
             dst = scale_b[:].rearrange("p (n m) -> p n m", m=8)[:, :, 4 * half : 4 * half + 4]
-            if half:
-                nc.vector.tensor_copy(out=dst, in_=sp[:].rearrange("p m n -> p n m"))
-            else:
-                nc.scalar.copy(out=dst, in_=sp[:].rearrange("p m n -> p n m"))
+            copy(eng, dst, sp[:].rearrange("p (m n) -> p n m", m=4))
 
-        def prep_x(g):
-            for t in range(4):
-                widen(g, t)
-                x_turn(g, t)
-                x_copy(g, t)
-            x_quant(g)
+        def cast_offset():
+            nc.scalar.copy(out=off_f[:], in_=off_rows[:])
 
-        def prep_b(n, e0="s", e1="s"):
+        def turn_offset():
+            off_ps = bank()
+            nc.tensor.transpose(off_ps[:, 0:P], off_f[:], ident[:])
+            nc.scalar.copy(out=off_cols[:], in_=off_ps[:, 0:FT])
+
+        c_int, c_codes, x_codes, b_codes, k_codes = {}, {}, {}, {}, {}
+        x_wide, x_tp, x_int, b_tp, b_int = {}, {}, {}, {}, {}
+
+        def c_inter(q, h, eng):
+            cint = pool.tile([P, 512, 4], BF16, bufs=BUFS["cint"], name="cint", align_bytes=64)
+            copy(eng, cint[:].rearrange("p (c i) t -> p c t i", i=4), c_raw[q, h][:].rearrange("p t (c i) -> p c t i", i=4))
+            c_int[q, h] = cint
+
+        def c_quant(q, h):
+            c_codes[q, h] = quantise(f"c{q}{h}", c_int[q, h][:].rearrange("p f t -> p (f t)"), 512)
+
+        def widen(g, t):
+            xw = pool.tile([P, K], BF16, bufs=BUFS["xw"], name="xw", tag="xw")
+            nc.vector.tensor_tensor(out=xw[:], in0=x_raw[g, t // 2][:, t % 2, :].bitcast(FP8), in1=scale_b[:], op=MULT)
+            x_wide[g, t] = xw
+
+        def x_turn(g, u, q):
+            tp = bank()
+            for e in range(2):
+                words = x_wide[g, 2 * u + e][:].bitcast(F32)
+                for w in range(2):
+                    i = 2 * e + w
+                    nc.tensor.transpose(tp[:, i * P : (i + 1) * P], words[:, 256 * q + w : 256 * (q + 1) : 2], ident[:])
+            x_tp[g, u, q] = tp
+
+        def x_copy(g, u, q, eng="s"):
+            if (u, q) == (0, 0):
+                xint = pool.tile([P, Q * 512 * 4], BF16, bufs=BUFS["xint"], name="xint", align_bytes=64)
+                x_int[g] = xint
+            first = 1024 * q + 512 * u
+            dst = x_int[g][:].bitcast(F32)[:, first : first + 512]
+            copy(eng, dst.rearrange("p (r i) -> p r i", i=4), x_tp[g, u, q][:].rearrange("p (i r) -> p r i", i=4))
+
+        def x_quant(g):
+            x_codes[g] = quantise(f"x{g}", x_int[g][:], Q * 512)
+
+        def b_turn(n, half):
+            words = b_raw[n][:].bitcast(F32)
+            tp = bank()
+            for gl in range(2):
+                g = 2 * half + gl
+                for w in range(2):
+                    i = 2 * gl + w
+                    nc.tensor.transpose(tp[:, i * P : (i + 1) * P], words[:, 256 * g + w : 256 * (g + 1) : 2], ident[:])
+            b_tp[n, half] = tp
+
+        def b_copy(n, half, eng="s"):
+            if half == 0:
+                bint = pool.tile([P, G * P * 4], BF16, bufs=BUFS["bint"], name="bint", align_bytes=64)
+                b_int[n] = bint
+            dst = b_int[n][:].bitcast(F32)[:, 512 * half : 512 * (half + 1)]
+            copy(eng, dst.rearrange("p (g r w) -> p g r w", g=2, w=2), b_tp[n, half][:].rearrange("p (g w r) -> p g r w", g=2, w=2))
+
+        def b_quant(n):
+            b_codes[n] = quantise(f"b{n}", b_int[n][:], G * P)
+
+        s_ps, tanh_t, k_wide, k_tp, k_int, v_ps = {}, {}, {}, {}, {}, {}
+
+        def sigma(g, ft):
+            ps = bank()
+            h, col = ft // 4, slice((ft % 4) * P, (ft % 4 + 1) * P)
+            xc, xs = x_codes[g]
+            for q in range(Q):
+                cc, cs = c_codes[q, h]
+                agents = slice(512 * q, 512 * (q + 1))
+                nc.tensor.matmul_mx(
+                    out=ps[:],
+                    lhsT=cc[:, col].bitcast(FP8X4),
+                    lhsT_scale=cs[:, col],
+                    rhs=xc[:, agents].bitcast(FP8X4),
+                    rhs_scale=xs[:, agents],
+                    start=(q == 0),
+                    stop=(q == Q - 1),
+                )
+            s_ps[g, ft] = ps
+
+        def tanh(g, ft):
+            th = pool.tile([P, 512], F32, bufs=1, name=f"th{g}{ft % BUFS['thmod']}")
+            nc.scalar.activation(out=th[:], in_=s_ps[g, ft][:], func=ACT.Tanh, bias=off_cols[:, ft : ft + 1])
+            tanh_t[g, ft] = th
+
+        def k_gain(g, ft):
+            kw = pool.tile([P, 512], BF16, bufs=BUFS["kw"], name="kw")
+            nc.vector.tensor_tensor(
+                out=kw[:].rearrange("f (u p e) -> f u p e", u=2, e=2),
+                in0=tanh_t[g, ft][:].rearrange("f (u p e) -> f u p e", u=2, e=2),
+                in1=gain_b[:, 512 * g : 512 * (g + 1)].rearrange("f (p u e) -> f u p e", u=2, e=2),
+                op=MULT,
+            )
+            k_wide[g, ft] = kw
+
+        def k_turn(g, ch):
+            tp = bank()
+            for i in range(FPC):
+                words = k_wide[g, ch * FPC + i][:].bitcast(F32)
+                for u in range(2):
+                    j = 2 * i + u
+                    nc.tensor.transpose(tp[:, j * P : (j + 1) * P], words[:, P * u : P * (u + 1)], ident[:])
+            k_tp[g, ch] = tp
+
+        def k_copy(g, ch, eng="s"):
+            kint = pool.tile([P, FC * 4], BF16, bufs=BUFS["kint"], name="kint", align_bytes=64)
+            dst = kint[:].bitcast(F32).rearrange("p (i f u) -> p i f u", i=FPC, u=2)
+            copy(eng, dst, k_tp[g, ch][:].rearrange("p (i u f) -> p i f u", i=FPC, u=2))
+            k_int[g, ch] = kint
+
+        def k_quant(g, ch):
+            k_codes[g, ch] = quantise(f"k{g}{ch}", k_int[g, ch][:], FC)
+
+        def node_tile(ps, ch, n):
+            bc, bs = b_codes[n]
+            for g in range(G):
+                kc, ks = k_codes[g, ch]
+                nodes = slice(P * g, P * (g + 1))
+                nc.tensor.matmul_mx(
+                    out=ps,
+                    lhsT=bc[:, nodes].bitcast(FP8X4),
+                    lhsT_scale=bs[:, nodes],
+                    rhs=kc[:].bitcast(FP8X4),
+                    rhs_scale=ks[:],
+                    start=(g == 0),
+                    stop=(g == G - 1),
+                )
+
+        def second(ch, pair):
+            ps = bank()
+            for i in range(2):
+                node_tile(ps[:, FC * i : FC * (i + 1)], ch, 2 * pair + i)
+            v_ps[ch, pair] = ps
+
+        def store(ch, pair, eng="s"):
+            vo = pool.tile([P, 2 * FC], F32, bufs=BUFS["xw"], name="vo", tag="xw")
+            copy(eng, vo[:], v_ps[ch, pair][:])
+            nc.sync.dma_start(
+                out=out[2 * pair * P : 2 * (pair + 1) * P, ch * FC : (ch + 1) * FC].rearrange("(i p) f -> p i f", i=2),
+                in_=vo[:].rearrange("p (i f) -> p i f", i=2),
+            )
+
+        def second1(ch, n):
+            ps = bank()
+            node_tile(ps[:, 0:FC], ch, n)
+            v_ps[ch, "single", n] = ps
+
+        def store1(ch, n, eng="s"):
+            vo = pool.tile([P, 2 * FC], F32, bufs=BUFS["xw"], name="vo", tag="xw")
+            copy(eng, vo[:, 0:FC], v_ps[ch, "single", n][:, 0:FC])
+            nc.sync.dma_start(out=out[n * P : (n + 1) * P, ch * FC : (ch + 1) * FC], in_=vo[:, 0:FC])
+
+        ctx.enter_context(tc.manual_schedule())
+        nc.gpsimd.memset(off_rows[:], 0.0)
+        nc.gpsimd.memset(warm[:], 0.0)
+        make_identity(nc, ident[:])
+        def x_pair(g, u):
+            for q in range(Q):
+                x_turn(g, u, q)
+            for q in range(Q):
+                x_copy(g, u, q)
+
+        def b_tile(n):
             for half in range(2):
                 b_turn(n, half)
-                b_copy(n, half, e1 if half else e0)
-            b_quant(n)
+            for half in range(2):
+                b_copy(n, half)
 
-        def ctrl(g, ch):
+        def surfaces(tiles):
+            for g, ft in tiles:
+                sigma(g, ft)
+            for g, ft in tiles:
+                tanh(g, ft)
+
+        def widen_pair(g, u):
+            widen(g, 2 * u)
+            widen(g, 2 * u + 1)
+
+        def gains(g, ch):
             for i in range(FPC):
                 k_gain(g, ch * FPC + i)
-            k_turn(g, ch)
-            k_copy(g, ch)
-            k_quant(g, ch)
 
-        def off_prep():
-            nc.scalar.copy(out=off_f[:], in_=off_rows[:])
-            off_ps = psum.tile([P, 4, P], F32, name="tp")
-            nc.tensor.transpose(off_ps[:, 0, :], off_f[:], ident[:])
-            nc.scalar.copy(out=off_cols[:], in_=off_ps[:, 0, 0:FT])
+        load_scale()
+        load_offset()
+        warm_tanh()
+        load_x(0, 0)
+        load_c(0, 0)
+        load_x(0, 1)
+        load_b(0)
+        load_c(1, 0)
+        load_b(1)
+        load_x(1, 0)
+        load_x(1, 1)
+        load_b(2)
+        load_c(0, 1)
+        cast_offset()
+        spread_scale(0, "v")
+        spread_scale(1, "s")
+        turn_offset()
+        c_inter(0, 0, "s")
+        load_b(3)
 
-        prep_b(0, "s", "v")
-        c_inter(0, 0, "v")
-        for t in range(4):
-            widen(0, t); x_turn(0, t); x_copy(0, t)
-        c_inter(1, 0, "s")
+        widen_pair(0, 0)
+        load_x(2, 0)
+        b_tile(0)
+        x_pair(0, 0)
+        widen_pair(0, 1)
+        load_x(2, 1)
+        load_b(4)
+        b_tile(1)
+        x_pair(0, 1)
+        widen_pair(1, 0)
+        b_tile(2)
+        x_pair(1, 0)
+        c_inter(1, 0, "v")
+        load_c(1, 1)
+        load_b(5)
+        load_x(3, 0)
         c_quant(0, 0)
         x_quant(0)
         c_quant(1, 0)
-        off_prep()
-        prep_b(1, "s", "s")
-        prep_b(2, "s", "s")
-        c_inter(0, 1, "v")
-        c_inter(1, 1, "s")
-        c_quant(0, 1)
-        c_quant(1, 1)
-        for g in range(G):
-            for ft in range(FT):
-                sigma(g, ft)
-                tanh(g, ft)
-            if g + 1 < G:
-                prep_x(g + 1)
-            ctrl(g, 0)
-            if g == 0:
-                load_x(3)[0]()
-            for n in {0: (3, 4), 1: (5, 6), 2: (7,), 3: ()}[g]:
-                prep_b(n, "s", "s")
-        for ch in range(1, CH):
-            for g in range(G):
-                ctrl(g, ch)
-            for pair in range(NT // 2):
-                second(ch - 1, pair, "s")
-        for pair in range(NT // 2):
-            second(CH - 1, pair, "s" if pair % 2 else "v")
+        b_tile(3)
+        for r in range(3, 7):
+            g, u = divmod(r, 2)
+            widen_pair(g, u)
+            if r == 3:
+                load_x(3, 1)
+                load_b(6)
+            first = 2 * (r - 3)
+            surfaces([(first // 4, first % 4), (first // 4, first % 4 + 1)])
+            x_pair(g, u)
+            if u == 0:
+                x_quant(g - 1)
+            if r in (4, 5):
+                c_inter(r - 4, 1, "v")
+            if r == 4:
+                load_b(7)
+                load_gain()
+            if r in (5, 6):
+                c_quant(r - 5, 1)
+            b_tile(r + 1)
+        widen_pair(3, 1)
+        surfaces([(2, 0), (2, 1)])
+        x_pair(3, 1)
+        gains(0, 0)
+        gains(1, 0)
+        surfaces([(2, 2), (2, 3)])
+        x_quant(3)
+
+        def turn_unit(i, engines="ss"):
+            ch, half = divmod(i, 2)
+            for g in (2 * half, 2 * half + 1):
+                k_turn(g, ch)
+            for g in (2 * half, 2 * half + 1):
+                k_copy(g, ch, engines[g % 2])
+
+        def gain_unit(i):
+            ch, half = divmod(i, 2)
+            gains(2 * half, ch)
+            gains(2 * half + 1, ch)
+
+        def quant_unit(i):
+            ch, half = divmod(i, 2)
+            k_quant(2 * half, ch)
+            k_quant(2 * half + 1, ch)
+
+        surfaces([(0, 4), (0, 5)])
+        turn_unit(0)
+        surfaces([(3, 0), (3, 1)])
+        gain_unit(1)
+        surfaces([(3, 2), (3, 3), (1, 4), (1, 5)])
+        quant_unit(0)
+        turn_unit(1)
+        gain_unit(2)
+        b_quant(0)
+        b_quant(1)
+        surfaces([(2, 4), (2, 5), (3, 4), (3, 5)])
+        quant_unit(1)
+        b_quant(2)
+        b_quant(3)
+        for h in range(8):
+            ch, half = divmod(h, 2)
+            if h + 2 < 8:
+                turn_unit(h + 2)
+            if h + 3 < 8:
+                gain_unit(h + 3)
+            if h == 0:
+                for n in range(4, 8):
+                    b_quant(n)
+            if h + 2 < 8:
+                quant_unit(h + 2)
+            for pair in (2 * half, 2 * half + 1):
+                second(ch, pair)
+                if h < 2:
+                    surfaces([(pair, 6), (pair, 7)])
+                store(ch, pair, "s" if h < 6 or pair % 2 else "v")

@@ -24,21 +24,31 @@ CH = 4
 FC = F // CH
 FPC = FC // P
 BANKS = 8
-BUFS = {"braw": 6, "cint": 2, "xw": 4, "xint": 2, "bint": 8, "thmod": 4, "kw": 8, "kint": 4, "xb": 4}
+BUFS = {"braw": 6, "cint": 2, "xw": 6, "xint": 2, "bint": 8, "thmod": 8, "kw": 8, "kint": 4, "xb": 4, "vo": 4}
+KIB = 1024
+AT_RAW = 0
+AT_KW, AT_KINT, AT_VO = AT_RAW, AT_RAW + 8 * KIB, AT_RAW + 16 * KIB
+AT_XB = AT_RAW + 24 * KIB
+AT_XW = AT_XB + 8 * KIB
+AT_XINT = AT_XW + 12 * KIB
+AT_BINT = AT_XINT + 16 * KIB
+AT_TH = AT_BINT + 32 * KIB
+AT_CINT = AT_TH + 56 * KIB
 
 
 def tile_networked_sliding_control_s7_kernel(tc, x_bytes, x_scale, c, offset, gain, bmat, out):
     nc = tc.nc
     with ExitStack() as ctx:
         const = ctx.enter_context(tc.tile_pool(name="const", bufs=1))
-        pool = ctx.enter_context(tc.tile_pool(name="work", bufs=2))
+        kept = ctx.enter_context(tc.tile_pool(name="kept", bufs=1))
+        pool = ctx.enter_context(tc.tile_pool(name="work", bufs=1))
         psum = ctx.enter_context(tc.psum_pool(name="psum", bufs=1))
 
         x_view = x_bytes.rearrange("(g p u e) k -> g u p e k", p=P, u=2, e=2)
         c_view = c.rearrange("(q p j) (h f) -> q h p j f", p=P, j=4, h=2)
         b_view = bmat.rearrange("(n p) m -> n p m", p=P)
         x_raw, c_raw, b_raw = {}, {}, {}
-        banks_taken = []
+        banks_taken, kept_widths = [], []
 
         def bank():
             tile = psum.tile([P, 512], F32, name=f"bank{len(banks_taken) % BANKS}")
@@ -52,23 +62,25 @@ def tile_networked_sliding_control_s7_kernel(tc, x_bytes, x_scale, c, offset, ga
                 nc.scalar.copy(out=dst, in_=src)
 
         def quantise(name, src, width):
-            codes = const.tile([P, width], U32, name=f"codes_{name}", align_bytes=256)
-            scales = const.tile([P, width], U8, name=f"scales_{name}", align_bytes=256)
+            first = 5 * sum(kept_widths)
+            kept_widths.append(width)
+            codes = kept.tile([P, width], U32, name=f"codes_{name}", align_bytes=256, offset=first)
+            scales = kept.tile([P, width], U8, name=f"scales_{name}", align_bytes=256, offset=first + 4 * width)
             nc.vector.quantize_mx(out=codes[:].bitcast(FP8X4), scales=scales[:], in_=src)
             return codes, scales
 
         def load_x(g, u):
-            xbytes = pool.tile([P, 2, K], U8, bufs=BUFS["xb"], name="xbytes")
+            xbytes = pool.tile([P, 2, K], U8, bufs=BUFS["xb"], name="xbytes", align_bytes=64, offset=AT_XB)
             nc.sync.dma_start(out=xbytes[:], in_=x_view[g, u])
             x_raw[g, u] = xbytes
 
         def load_c(q, h):
-            raw = pool.tile([P, 4, 512], BF16, bufs=BUFS["braw"], name="raw")
+            raw = pool.tile([P, 4, 512], BF16, bufs=BUFS["braw"], name="raw", align_bytes=64, offset=AT_RAW)
             nc.sync.dma_start(out=raw[:], in_=c_view[q, h])
             c_raw[q, h] = raw
 
         def load_b(n):
-            raw = pool.tile([P, M], BF16, bufs=BUFS["braw"], name="raw")
+            raw = pool.tile([P, M], BF16, bufs=BUFS["braw"], name="raw", align_bytes=64, offset=AT_RAW)
             nc.sync.dma_start(out=raw[:], in_=b_view[n])
             b_raw[n] = raw
 
@@ -78,12 +90,12 @@ def tile_networked_sliding_control_s7_kernel(tc, x_bytes, x_scale, c, offset, ga
         warm_out = const.tile([P, 1], F32)
         scale_b = const.tile([P, K], F32)
         gain_b = const.tile([P, M], BF16)
-        scale_v = const.tile([P, 8], F32)
+        scale_v = const.tile([P, Q, 4], F32)
         off_f = const.tile([P, P], F32)
         off_cols = const.tile([P, FT], F32)
 
         def load_scale():
-            nc.scalar.dma_start(out=scale_v[:], in_=x_scale.rearrange("o (p m) -> (o p) m", m=8))
+            nc.scalar.dma_start(out=scale_v[:], in_=x_scale.rearrange("o (q p m) -> p (o q) m", p=P, m=4))
 
         def load_offset():
             nc.scalar.dma_start(out=off_rows[0:FT, :], in_=offset.rearrange("(c p) -> c p", p=P))
@@ -94,12 +106,11 @@ def tile_networked_sliding_control_s7_kernel(tc, x_bytes, x_scale, c, offset, ga
         def warm_tanh():
             nc.scalar.activation(out=warm_out[:], in_=warm[:], func=ACT.Tanh)
 
-        def spread_scale(half, eng):
+        def spread_scale(q, eng):
             sp = bank()
-            for i in range(4):
-                col = 4 * half + i
-                nc.tensor.transpose(sp[:, i * P : (i + 1) * P], scale_v[:, col : col + 1].to_broadcast([P, P]), ident[:])
-            dst = scale_b[:].rearrange("p (n m) -> p n m", m=8)[:, :, 4 * half : 4 * half + 4]
+            for m in range(4):
+                nc.tensor.transpose(sp[:, m * P : (m + 1) * P], scale_v[:, q, m : m + 1].to_broadcast([P, P]), ident[:])
+            dst = scale_b[:, 512 * q : 512 * (q + 1)].rearrange("p (n m) -> p n m", m=4)
             copy(eng, dst, sp[:].rearrange("p (m n) -> p n m", m=4))
 
         def cast_offset():
@@ -114,7 +125,7 @@ def tile_networked_sliding_control_s7_kernel(tc, x_bytes, x_scale, c, offset, ga
         x_wide, x_tp, x_int, b_tp, b_int = {}, {}, {}, {}, {}
 
         def c_inter(q, h, eng):
-            cint = pool.tile([P, 512, 4], BF16, bufs=BUFS["cint"], name="cint", align_bytes=64)
+            cint = pool.tile([P, 512, 4], BF16, bufs=BUFS["cint"], name="cint", align_bytes=64, offset=AT_CINT)
             copy(eng, cint[:].rearrange("p (c i) t -> p c t i", i=4), c_raw[q, h][:].rearrange("p t (c i) -> p c t i", i=4))
             c_int[q, h] = cint
 
@@ -122,9 +133,18 @@ def tile_networked_sliding_control_s7_kernel(tc, x_bytes, x_scale, c, offset, ga
             c_codes[q, h] = quantise(f"c{q}{h}", c_int[q, h][:].rearrange("p f t -> p (f t)"), 512)
 
         def widen(g, t):
-            xw = pool.tile([P, K], BF16, bufs=BUFS["xw"], name="xw", tag="xw")
+            xw = pool.tile([P, K], BF16, bufs=BUFS["xw"], name="xw", align_bytes=64, offset=AT_XW)
             nc.vector.tensor_tensor(out=xw[:], in0=x_raw[g, t // 2][:, t % 2, :].bitcast(FP8), in1=scale_b[:], op=MULT)
             x_wide[g, t] = xw
+
+        def widen_half(g, t, q):
+            if q == 0:
+                xw = pool.tile([P, K], BF16, bufs=BUFS["xw"], name="xw", align_bytes=64, offset=AT_XW)
+                x_wide[g, t] = xw
+            states = slice(512 * q, 512 * (q + 1))
+            nc.vector.tensor_tensor(
+                out=x_wide[g, t][:, states], in0=x_raw[g, t // 2][:, t % 2, states].bitcast(FP8), in1=scale_b[:, states], op=MULT
+            )
 
         def x_turn(g, u, q):
             tp = bank()
@@ -137,7 +157,7 @@ def tile_networked_sliding_control_s7_kernel(tc, x_bytes, x_scale, c, offset, ga
 
         def x_copy(g, u, q, eng="s"):
             if (u, q) == (0, 0):
-                xint = pool.tile([P, Q * 512 * 4], BF16, bufs=BUFS["xint"], name="xint", align_bytes=64)
+                xint = pool.tile([P, Q * 512 * 4], BF16, bufs=BUFS["xint"], name="xint", align_bytes=64, offset=AT_XINT)
                 x_int[g] = xint
             first = 1024 * q + 512 * u
             dst = x_int[g][:].bitcast(F32)[:, first : first + 512]
@@ -158,7 +178,7 @@ def tile_networked_sliding_control_s7_kernel(tc, x_bytes, x_scale, c, offset, ga
 
         def b_copy(n, half, eng="s"):
             if half == 0:
-                bint = pool.tile([P, G * P * 4], BF16, bufs=BUFS["bint"], name="bint", align_bytes=64)
+                bint = pool.tile([P, G * P * 4], BF16, bufs=BUFS["bint"], name="bint", align_bytes=64, offset=AT_BINT)
                 b_int[n] = bint
             dst = b_int[n][:].bitcast(F32)[:, 512 * half : 512 * (half + 1)]
             copy(eng, dst.rearrange("p (g r w) -> p g r w", g=2, w=2), b_tp[n, half][:].rearrange("p (g w r) -> p g r w", g=2, w=2))
@@ -187,12 +207,12 @@ def tile_networked_sliding_control_s7_kernel(tc, x_bytes, x_scale, c, offset, ga
             s_ps[g, ft] = ps
 
         def tanh(g, ft):
-            th = pool.tile([P, 512], F32, bufs=1, name=f"th{g}{ft % BUFS['thmod']}")
+            th = pool.tile([P, 512], F32, name=f"th{g}{ft}", align_bytes=64, offset=AT_TH + 2 * KIB * len(tanh_t))
             nc.scalar.activation(out=th[:], in_=s_ps[g, ft][:], func=ACT.Tanh, bias=off_cols[:, ft : ft + 1])
             tanh_t[g, ft] = th
 
         def k_gain(g, ft):
-            kw = pool.tile([P, 512], BF16, bufs=BUFS["kw"], name="kw")
+            kw = pool.tile([P, 512], BF16, bufs=BUFS["kw"], name="kw", align_bytes=64, offset=AT_KW)
             nc.vector.tensor_tensor(
                 out=kw[:].rearrange("f (u p e) -> f u p e", u=2, e=2),
                 in0=tanh_t[g, ft][:].rearrange("f (u p e) -> f u p e", u=2, e=2),
@@ -211,7 +231,7 @@ def tile_networked_sliding_control_s7_kernel(tc, x_bytes, x_scale, c, offset, ga
             k_tp[g, ch] = tp
 
         def k_copy(g, ch, eng="s"):
-            kint = pool.tile([P, FC * 4], BF16, bufs=BUFS["kint"], name="kint", align_bytes=64)
+            kint = pool.tile([P, FC * 4], BF16, bufs=BUFS["kint"], name="kint", align_bytes=64, offset=AT_KINT)
             dst = kint[:].bitcast(F32).rearrange("p (i f u) -> p i f u", i=FPC, u=2)
             copy(eng, dst, k_tp[g, ch][:].rearrange("p (i u f) -> p i f u", i=FPC, u=2))
             k_int[g, ch] = kint
@@ -241,7 +261,7 @@ def tile_networked_sliding_control_s7_kernel(tc, x_bytes, x_scale, c, offset, ga
             v_ps[ch, pair] = ps
 
         def store(ch, pair, eng="s"):
-            vo = pool.tile([P, 2 * FC], F32, bufs=BUFS["xw"], name="vo", tag="xw")
+            vo = pool.tile([P, 2 * FC], F32, bufs=BUFS["vo"], name="vo", align_bytes=64, offset=AT_VO)
             copy(eng, vo[:], v_ps[ch, pair][:])
             nc.sync.dma_start(
                 out=out[2 * pair * P : 2 * (pair + 1) * P, ch * FC : (ch + 1) * FC].rearrange("(i p) f -> p i f", i=2),
@@ -254,7 +274,7 @@ def tile_networked_sliding_control_s7_kernel(tc, x_bytes, x_scale, c, offset, ga
             v_ps[ch, "single", n] = ps
 
         def store1(ch, n, eng="s"):
-            vo = pool.tile([P, 2 * FC], F32, bufs=BUFS["xw"], name="vo", tag="xw")
+            vo = pool.tile([P, 2 * FC], F32, bufs=BUFS["vo"], name="vo", align_bytes=64, offset=AT_VO)
             copy(eng, vo[:, 0:FC], v_ps[ch, "single", n][:, 0:FC])
             nc.sync.dma_start(out=out[n * P : (n + 1) * P, ch * FC : (ch + 1) * FC], in_=vo[:, 0:FC])
 
@@ -288,72 +308,6 @@ def tile_networked_sliding_control_s7_kernel(tc, x_bytes, x_scale, c, offset, ga
             for i in range(FPC):
                 k_gain(g, ch * FPC + i)
 
-        load_scale()
-        load_offset()
-        warm_tanh()
-        load_x(0, 0)
-        load_c(0, 0)
-        load_x(0, 1)
-        load_b(0)
-        load_c(1, 0)
-        load_b(1)
-        load_x(1, 0)
-        load_x(1, 1)
-        load_b(2)
-        load_c(0, 1)
-        cast_offset()
-        spread_scale(0, "v")
-        spread_scale(1, "s")
-        turn_offset()
-        c_inter(0, 0, "s")
-        load_b(3)
-
-        widen_pair(0, 0)
-        load_x(2, 0)
-        b_tile(0)
-        x_pair(0, 0)
-        widen_pair(0, 1)
-        load_x(2, 1)
-        load_b(4)
-        b_tile(1)
-        x_pair(0, 1)
-        widen_pair(1, 0)
-        b_tile(2)
-        x_pair(1, 0)
-        c_inter(1, 0, "v")
-        load_c(1, 1)
-        load_b(5)
-        load_x(3, 0)
-        c_quant(0, 0)
-        x_quant(0)
-        c_quant(1, 0)
-        b_tile(3)
-        for r in range(3, 7):
-            g, u = divmod(r, 2)
-            widen_pair(g, u)
-            if r == 3:
-                load_x(3, 1)
-                load_b(6)
-            first = 2 * (r - 3)
-            surfaces([(first // 4, first % 4), (first // 4, first % 4 + 1)])
-            x_pair(g, u)
-            if u == 0:
-                x_quant(g - 1)
-            if r in (4, 5):
-                c_inter(r - 4, 1, "v")
-            if r == 4:
-                load_b(7)
-                load_gain()
-            if r in (5, 6):
-                c_quant(r - 5, 1)
-            b_tile(r + 1)
-        widen_pair(3, 1)
-        surfaces([(2, 0), (2, 1)])
-        x_pair(3, 1)
-        gains(0, 0)
-        gains(1, 0)
-        surfaces([(2, 2), (2, 3)])
-        x_quant(3)
 
         def turn_unit(i, engines="ss"):
             ch, half = divmod(i, 2)
@@ -372,33 +326,107 @@ def tile_networked_sliding_control_s7_kernel(tc, x_bytes, x_scale, c, offset, ga
             k_quant(2 * half, ch)
             k_quant(2 * half + 1, ch)
 
-        surfaces([(0, 4), (0, 5)])
+
+        load_scale()
+        load_offset()
+        warm_tanh()
+        load_x(0, 0)
+        load_b(0)
+        load_b(1)
+        load_x(0, 1)
+        load_b(2)
+        load_x(1, 0)
+        load_b(3)
+        load_x(1, 1)
+        load_b(4)
+        load_c(0, 0)
+        cast_offset()
+        spread_scale(0, "v")
+        spread_scale(1, "s")
+        turn_offset()
+        for q in range(Q):
+            for t in range(2):
+                widen_half(0, t, q)
+        b_tile(0)
+        load_c(1, 0)
+        b_tile(1)
+        load_b(5)
+        for r in range(4):
+            if r:
+                widen_pair(r // 2, r % 2)
+            x_pair(r // 2, r % 2)
+            b_tile(r + 2)
+            if r < 2:
+                load_b(6 + r)
+            else:
+                load_x(2, r - 2)
+                load_c(r - 2, 1)
+        load_x(3, 0)
+        load_x(3, 1)
+        load_gain()
+        c_inter(0, 0, "v")
+        c_inter(1, 0, "v")
+        x_quant(0)
+        c_quant(0, 0)
+        c_quant(1, 0)
+        b_tile(6)
+        b_tile(7)
+        x_quant(1)
+        widen_pair(2, 0)
+        c_inter(0, 1, "v")
+        c_inter(1, 1, "v")
+        surfaces([(g, ft) for g in range(2) for ft in range(4)])
+        x_pair(2, 0)
+        c_quant(0, 1)
+        c_quant(1, 1)
+        widen_pair(2, 1)
+        widen_pair(3, 0)
+        surfaces([(0, ft) for ft in range(4, 8)])
+        x_pair(2, 1)
+        gains(0, 0)
+        surfaces([(1, 4), (1, 5)])
+        x_quant(2)
+        x_pair(3, 0)
+        widen_pair(3, 1)
+        surfaces([(1, 6), (1, 7), (2, 0), (2, 1)])
+        gains(1, 0)
+        x_pair(3, 1)
         turn_unit(0)
-        surfaces([(3, 0), (3, 1)])
-        gain_unit(1)
-        surfaces([(3, 2), (3, 3), (1, 4), (1, 5)])
-        quant_unit(0)
-        turn_unit(1)
-        gain_unit(2)
         b_quant(0)
         b_quant(1)
-        surfaces([(2, 4), (2, 5), (3, 4), (3, 5)])
-        quant_unit(1)
+        x_quant(3)
+        surfaces([(2, ft) for ft in range(2, 6)])
+        gains(2, 0)
+        quant_unit(0)
+        gains(0, 1)
+        surfaces([(3, ft) for ft in range(6)])
+        gains(3, 0)
+        gains(1, 1)
+        surfaces([(2, 6), (2, 7)])
+        turn_unit(1)
+        turn_unit(2)
         b_quant(2)
         b_quant(3)
-        for h in range(8):
+        gains(2, 1)
+        surfaces([(3, 6), (3, 7)])
+        quant_unit(1)
+        gains(3, 1)
+        for n in range(4, 8):
+            b_quant(n)
+        quant_unit(2)
+        for h in range(6):
             ch, half = divmod(h, 2)
-            if h + 2 < 8:
-                turn_unit(h + 2)
-            if h + 3 < 8:
-                gain_unit(h + 3)
-            if h == 0:
-                for n in range(4, 8):
-                    b_quant(n)
-            if h + 2 < 8:
-                quant_unit(h + 2)
+            if h + 4 < 8:
+                gain_unit(h + 4)
             for pair in (2 * half, 2 * half + 1):
                 second(ch, pair)
-                if h < 2:
-                    surfaces([(pair, 6), (pair, 7)])
-                store(ch, pair, "s" if h < 6 or pair % 2 else "v")
+                store(ch, pair)
+            if h + 3 < 8:
+                turn_unit(h + 3)
+                quant_unit(h + 3)
+        for pair in range(3):
+            second(3, pair)
+            store(3, pair, "s")
+        for n in (6, 7):
+            second1(3, n)
+            store1(3, n, "s" if n % 2 else "v")

@@ -24,12 +24,13 @@ CH = 4
 FC = F // CH
 FPC = FC // P
 BANKS = 8
-BUFS = {"braw": 6, "cint": 2, "xw": 6, "xint": 2, "bint": 8, "thmod": 8, "kw": 8, "kint": 4, "xb": 4, "vo": 4}
+BUFS = {"braw": 6, "cint": 2, "xw": 6, "xint": 2, "bint": 8, "thmod": 8, "kw": 16, "kint": 4, "xb": 4, "vo": 6}
 KIB = 1024
 AT_RAW = 0
-AT_KW, AT_KINT, AT_VO = AT_RAW, AT_RAW + 8 * KIB, AT_RAW + 16 * KIB
+AT_KW, AT_KINT = AT_RAW, AT_RAW + 16 * KIB
 AT_XB = AT_RAW + 24 * KIB
 AT_XW = AT_XB + 8 * KIB
+AT_VO = AT_XW
 AT_XINT = AT_XW + 12 * KIB
 AT_BINT = AT_XINT + 16 * KIB
 AT_TH = AT_BINT + 32 * KIB
@@ -82,7 +83,12 @@ def tile_networked_sliding_control_s7_kernel(tc, x_bytes, x_scale, c, offset, ga
         def load_b(n):
             raw = pool.tile([P, M], BF16, bufs=BUFS["braw"], name="raw", align_bytes=64, offset=AT_RAW)
             nc.sync.dma_start(out=raw[:], in_=b_view[n])
-            b_raw[n] = raw
+            b_raw[n] = [raw[:, 0 : M // 2], raw[:, M // 2 : M]]
+
+        def load_b_half(n, half):
+            raw = pool.tile([P, M // 2], BF16, name=f"raw_half{half}", align_bytes=64, offset=AT_TH + 2 * KIB * half)
+            nc.sync.dma_start(out=raw[:], in_=b_view[n][:, half * M // 2 : (half + 1) * M // 2])
+            b_raw.setdefault(n, []).append(raw[:])
 
         ident = const.tile([P, P], F32)
         off_rows = const.tile([P, P], BF16)
@@ -167,13 +173,12 @@ def tile_networked_sliding_control_s7_kernel(tc, x_bytes, x_scale, c, offset, ga
             x_codes[g] = quantise(f"x{g}", x_int[g][:], Q * 512)
 
         def b_turn(n, half):
-            words = b_raw[n][:].bitcast(F32)
+            words = b_raw[n][half].bitcast(F32)
             tp = bank()
             for gl in range(2):
-                g = 2 * half + gl
                 for w in range(2):
                     i = 2 * gl + w
-                    nc.tensor.transpose(tp[:, i * P : (i + 1) * P], words[:, 256 * g + w : 256 * (g + 1) : 2], ident[:])
+                    nc.tensor.transpose(tp[:, i * P : (i + 1) * P], words[:, 256 * gl + w : 256 * (gl + 1) : 2], ident[:])
             b_tp[n, half] = tp
 
         def b_copy(n, half, eng="s"):
@@ -330,16 +335,18 @@ def tile_networked_sliding_control_s7_kernel(tc, x_bytes, x_scale, c, offset, ga
         load_scale()
         load_offset()
         warm_tanh()
+        load_b_half(0, 0)
         load_x(0, 0)
-        load_b(0)
+        load_b_half(0, 1)
         load_b(1)
         load_x(0, 1)
         load_b(2)
         load_x(1, 0)
-        load_b(3)
-        load_x(1, 1)
-        load_b(4)
         load_c(0, 0)
+        load_b(3)
+        load_c(1, 0)
+        load_b(4)
+        load_x(1, 1)
         cast_offset()
         spread_scale(0, "v")
         spread_scale(1, "s")
@@ -348,71 +355,76 @@ def tile_networked_sliding_control_s7_kernel(tc, x_bytes, x_scale, c, offset, ga
             for t in range(2):
                 widen_half(0, t, q)
         b_tile(0)
-        load_c(1, 0)
         b_tile(1)
         load_b(5)
-        for r in range(4):
+        for r in range(3):
             if r:
                 widen_pair(r // 2, r % 2)
             x_pair(r // 2, r % 2)
             b_tile(r + 2)
             if r < 2:
-                load_b(6 + r)
-            else:
-                load_x(2, r - 2)
-                load_c(r - 2, 1)
-        load_x(3, 0)
-        load_x(3, 1)
-        load_gain()
+                load_c(r, 1)
         c_inter(0, 0, "v")
         c_inter(1, 0, "v")
+        load_b(6)
+        load_x(2, 0)
+        load_x(2, 1)
+        load_b(7)
         x_quant(0)
         c_quant(0, 0)
         c_quant(1, 0)
-        b_tile(6)
-        b_tile(7)
-        x_quant(1)
-        widen_pair(2, 0)
+        b_tile(5)
+        widen_pair(1, 1)
+        load_x(3, 0)
+        load_x(3, 1)
+        load_gain()
         c_inter(0, 1, "v")
         c_inter(1, 1, "v")
-        surfaces([(g, ft) for g in range(2) for ft in range(4)])
-        x_pair(2, 0)
+        surfaces([(0, ft) for ft in range(4)])
+        x_pair(1, 1)
+        b_tile(6)
         c_quant(0, 1)
         c_quant(1, 1)
+        x_quant(1)
+        widen_pair(2, 0)
         widen_pair(2, 1)
-        widen_pair(3, 0)
         surfaces([(0, ft) for ft in range(4, 8)])
+        surfaces([(1, ft) for ft in range(2)])
+        b_tile(7)
+        x_pair(2, 0)
+        widen_pair(3, 0)
+        surfaces([(1, ft) for ft in range(2, 4)])
         x_pair(2, 1)
-        gains(0, 0)
-        surfaces([(1, 4), (1, 5)])
-        x_quant(2)
-        x_pair(3, 0)
         widen_pair(3, 1)
-        surfaces([(1, 6), (1, 7), (2, 0), (2, 1)])
-        gains(1, 0)
+        x_quant(2)
+        gains(0, 0)
+        surfaces([(1, ft) for ft in range(4, 8)])
+        x_pair(3, 0)
         x_pair(3, 1)
-        turn_unit(0)
+        surfaces([(2, ft) for ft in range(4)])
+        gains(1, 0)
+        gains(0, 1)
+        x_quant(3)
+        gains(2, 0)
+        surfaces([(2, 4), (2, 5)])
+        surfaces([(3, ft) for ft in range(4)])
         b_quant(0)
         b_quant(1)
-        x_quant(3)
-        surfaces([(2, ft) for ft in range(2, 6)])
-        gains(2, 0)
-        quant_unit(0)
-        gains(0, 1)
-        surfaces([(3, ft) for ft in range(6)])
-        gains(3, 0)
         gains(1, 1)
+        gains(3, 0)
         surfaces([(2, 6), (2, 7)])
+        turn_unit(0)
         turn_unit(1)
-        turn_unit(2)
         b_quant(2)
         b_quant(3)
         gains(2, 1)
-        surfaces([(3, 6), (3, 7)])
+        surfaces([(3, ft) for ft in range(4, 8)])
+        quant_unit(0)
         quant_unit(1)
         gains(3, 1)
         for n in range(4, 8):
             b_quant(n)
+        turn_unit(2)
         quant_unit(2)
         for h in range(6):
             ch, half = divmod(h, 2)

@@ -24,7 +24,7 @@ CH = 4
 FC = F // CH
 FPC = FC // P
 BANKS = 8
-BUFS = {"braw": 6, "cint": 2, "xw": 6, "xint": 2, "bint": 8, "thmod": 8, "kw": 16, "kint": 4, "xb": 4, "vo": 6}
+BUFS = {"braw": 6, "cint": 2, "xw": 6, "xint": 2, "bint": 8, "thmod": 8, "kw": 16, "kint": 4, "xb": 4, "vo": 12}
 KIB = 1024
 AT_RAW = 0
 AT_KW, AT_KINT = AT_RAW, AT_RAW + 16 * KIB
@@ -73,7 +73,13 @@ def tile_networked_sliding_control_s7_kernel(tc, x_bytes, x_scale, c, offset, ga
         def load_x(g, u):
             xbytes = pool.tile([P, 2, K], U8, bufs=BUFS["xb"], name="xbytes", align_bytes=64, offset=AT_XB)
             nc.sync.dma_start(out=xbytes[:], in_=x_view[g, u])
-            x_raw[g, u] = xbytes
+            x_raw[g, u] = xbytes[:]
+
+        def load_xg(g):
+            xgroup = pool.tile([P, 2, 2, K], U8, name=f"xbytes_group{g}", align_bytes=64, offset=AT_XB + 4 * KIB * (g % 2))
+            nc.sync.dma_start(out=xgroup[:].rearrange("p u e k -> p (u e k)"), in_=x_bytes.rearrange("(g p t) k -> g p (t k)", p=P, t=4)[g])
+            for u in range(2):
+                x_raw[g, u] = xgroup[:, u]
 
         def load_c(q, h):
             raw = pool.tile([P, 4, 512], BF16, bufs=BUFS["braw"], name="raw", align_bytes=64, offset=AT_RAW)
@@ -92,8 +98,6 @@ def tile_networked_sliding_control_s7_kernel(tc, x_bytes, x_scale, c, offset, ga
 
         ident = const.tile([P, P], F32)
         off_rows = const.tile([P, P], BF16)
-        warm = const.tile([P, 1], F32)
-        warm_out = const.tile([P, 1], F32)
         scale_b = const.tile([P, K], F32)
         gain_b = const.tile([P, M], BF16)
         scale_v = const.tile([P, Q, 4], F32)
@@ -108,9 +112,6 @@ def tile_networked_sliding_control_s7_kernel(tc, x_bytes, x_scale, c, offset, ga
 
         def load_gain():
             nc.sync.dma_start(out=gain_b[:], in_=gain.partition_broadcast(P))
-
-        def warm_tanh():
-            nc.scalar.activation(out=warm_out[:], in_=warm[:], func=ACT.Tanh)
 
         def spread_scale(q, eng):
             sp = bank()
@@ -131,12 +132,14 @@ def tile_networked_sliding_control_s7_kernel(tc, x_bytes, x_scale, c, offset, ga
         x_wide, x_tp, x_int, b_tp, b_int = {}, {}, {}, {}, {}
 
         def c_inter(q, h, eng):
-            cint = pool.tile([P, 512, 4], BF16, bufs=BUFS["cint"], name="cint", align_bytes=64, offset=AT_CINT)
-            copy(eng, cint[:].rearrange("p (c i) t -> p c t i", i=4), c_raw[q, h][:].rearrange("p t (c i) -> p c t i", i=4))
-            c_int[q, h] = cint
+            if q == 0:
+                cint = pool.tile([P, Q * 512 * 4], BF16, name="cint", align_bytes=64, offset=AT_CINT)
+                c_int[h] = cint
+            dst = c_int[h][:, 2048 * q : 2048 * (q + 1)].rearrange("p (c i t) -> p c t i", i=4, t=4)
+            copy(eng, dst, c_raw[q, h][:].rearrange("p t (c i) -> p c t i", i=4))
 
-        def c_quant(q, h):
-            c_codes[q, h] = quantise(f"c{q}{h}", c_int[q, h][:].rearrange("p f t -> p (f t)"), 512)
+        def quant_c(h):
+            c_codes[h] = quantise(f"c{h}", c_int[h][:], Q * 512)
 
         def widen(g, t):
             xw = pool.tile([P, K], BF16, bufs=BUFS["xw"], name="xw", align_bytes=64, offset=AT_XW)
@@ -182,23 +185,24 @@ def tile_networked_sliding_control_s7_kernel(tc, x_bytes, x_scale, c, offset, ga
             b_tp[n, half] = tp
 
         def b_copy(n, half, eng="s"):
-            if half == 0:
-                bint = pool.tile([P, G * P * 4], BF16, bufs=BUFS["bint"], name="bint", align_bytes=64, offset=AT_BINT)
-                b_int[n] = bint
-            dst = b_int[n][:].bitcast(F32)[:, 512 * half : 512 * (half + 1)]
+            if n % 2 == 0 and half == 0:
+                bint = pool.tile([P, 2 * G * P * 4], BF16, bufs=NT // 2, name="bint", align_bytes=64, offset=AT_BINT)
+                b_int[n // 2] = bint
+            first = 1024 * (n % 2) + 512 * half
+            dst = b_int[n // 2][:].bitcast(F32)[:, first : first + 512]
             copy(eng, dst.rearrange("p (g r w) -> p g r w", g=2, w=2), b_tp[n, half][:].rearrange("p (g w r) -> p g r w", g=2, w=2))
 
-        def b_quant(n):
-            b_codes[n] = quantise(f"b{n}", b_int[n][:], G * P)
+        def quant_b(pair):
+            b_codes[pair] = quantise(f"b{pair}", b_int[pair][:], 2 * G * P)
 
         s_ps, tanh_t, k_wide, k_tp, k_int, v_ps = {}, {}, {}, {}, {}, {}
 
         def sigma(g, ft):
             ps = bank()
-            h, col = ft // 4, slice((ft % 4) * P, (ft % 4 + 1) * P)
             xc, xs = x_codes[g]
+            cc, cs = c_codes[ft // 4]
             for q in range(Q):
-                cc, cs = c_codes[q, h]
+                col = slice(512 * q + (ft % 4) * P, 512 * q + (ft % 4 + 1) * P)
                 agents = slice(512 * q, 512 * (q + 1))
                 nc.tensor.matmul_mx(
                     out=ps[:],
@@ -236,57 +240,51 @@ def tile_networked_sliding_control_s7_kernel(tc, x_bytes, x_scale, c, offset, ga
             k_tp[g, ch] = tp
 
         def k_copy(g, ch, eng="s"):
-            kint = pool.tile([P, FC * 4], BF16, bufs=BUFS["kint"], name="kint", align_bytes=64, offset=AT_KINT)
-            dst = kint[:].bitcast(F32).rearrange("p (i f u) -> p i f u", i=FPC, u=2)
-            copy(eng, dst, k_tp[g, ch][:].rearrange("p (i u f) -> p i f u", i=FPC, u=2))
-            k_int[g, ch] = kint
+            if g % 2 == 0:
+                kint = pool.tile([P, 2 * FC * 4], BF16, bufs=BUFS["kint"] // 2, name="kint", align_bytes=64, offset=AT_KINT)
+                k_int[g // 2, ch] = kint
+            dst = k_int[g // 2, ch][:].bitcast(F32)[:, 512 * (g % 2) : 512 * (g % 2 + 1)]
+            copy(eng, dst.rearrange("p (i f u) -> p i f u", i=FPC, u=2), k_tp[g, ch][:].rearrange("p (i u f) -> p i f u", i=FPC, u=2))
 
-        def k_quant(g, ch):
-            k_codes[g, ch] = quantise(f"k{g}{ch}", k_int[g, ch][:], FC)
+        def quant_k(unit):
+            ch, half = divmod(unit, 2)
+            k_codes[half, ch] = quantise(f"k{unit}", k_int[half, ch][:], 2 * FC)
 
-        def node_tile(ps, ch, n):
-            bc, bs = b_codes[n]
-            for g in range(G):
-                kc, ks = k_codes[g, ch]
-                nodes = slice(P * g, P * (g + 1))
-                nc.tensor.matmul_mx(
-                    out=ps,
-                    lhsT=bc[:, nodes].bitcast(FP8X4),
-                    lhsT_scale=bs[:, nodes],
-                    rhs=kc[:].bitcast(FP8X4),
-                    rhs_scale=ks[:],
-                    start=(g == 0),
-                    stop=(g == G - 1),
-                )
+        def nodes_part(ch, nodes, groups, first=0, width=FC):
+            if groups[0] == 0:
+                v_ps[ch, nodes, first] = bank()
+            ps = v_ps[ch, nodes, first]
+            for g in groups:
+                kc, ks = k_codes[g // 2, ch]
+                cols = slice(FC * (g % 2) + first, FC * (g % 2) + first + width)
+                for i, n in enumerate(nodes):
+                    bc, bs = b_codes[n // 2]
+                    rows = slice(512 * (n % 2) + P * g, 512 * (n % 2) + P * (g + 1))
+                    nc.tensor.matmul_mx(
+                        out=ps[:, width * i : width * (i + 1)],
+                        lhsT=bc[:, rows].bitcast(FP8X4),
+                        lhsT_scale=bs[:, rows],
+                        rhs=kc[:, cols].bitcast(FP8X4),
+                        rhs_scale=ks[:, cols],
+                        start=(g == 0 and i == 0),
+                        stop=(g == G - 1 and i == len(nodes) - 1),
+                    )
 
-        def second(ch, pair):
-            ps = bank()
-            for i in range(2):
-                node_tile(ps[:, FC * i : FC * (i + 1)], ch, 2 * pair + i)
-            v_ps[ch, pair] = ps
-
-        def store(ch, pair, eng="s"):
+        def store_nodes(ch, nodes, eng="s", first=0, width=FC):
             vo = pool.tile([P, 2 * FC], F32, bufs=BUFS["vo"], name="vo", align_bytes=64, offset=AT_VO)
-            copy(eng, vo[:], v_ps[ch, pair][:])
+            used = width * len(nodes)
+            copy(eng, vo[:, 0:used], v_ps[ch, nodes, first][:, 0:used])
+            rows = slice(nodes[0] * P, (nodes[-1] + 1) * P)
+            cols = slice(ch * FC + first, ch * FC + first + width)
             nc.sync.dma_start(
-                out=out[2 * pair * P : 2 * (pair + 1) * P, ch * FC : (ch + 1) * FC].rearrange("(i p) f -> p i f", i=2),
-                in_=vo[:].rearrange("p (i f) -> p i f", i=2),
+                out=out[rows, cols].rearrange("(i p) f -> p i f", p=P),
+                in_=vo[:, 0:used].rearrange("p (i f) -> p i f", f=width),
             )
 
-        def second1(ch, n):
-            ps = bank()
-            node_tile(ps[:, 0:FC], ch, n)
-            v_ps[ch, "single", n] = ps
-
-        def store1(ch, n, eng="s"):
-            vo = pool.tile([P, 2 * FC], F32, bufs=BUFS["vo"], name="vo", align_bytes=64, offset=AT_VO)
-            copy(eng, vo[:, 0:FC], v_ps[ch, "single", n][:, 0:FC])
-            nc.sync.dma_start(out=out[n * P : (n + 1) * P, ch * FC : (ch + 1) * FC], in_=vo[:, 0:FC])
-
         ctx.enter_context(tc.manual_schedule())
-        nc.gpsimd.memset(off_rows[:], 0.0)
-        nc.gpsimd.memset(warm[:], 0.0)
-        make_identity(nc, ident[:])
+        nc.vector.memset(ident[:], 0.0)
+        make_identity(nc, ident[:], nomemset=True)
+        nc.vector.memset(off_rows[:], 0.0)
         def x_pair(g, u):
             for q in range(Q):
                 x_turn(g, u, q)
@@ -313,28 +311,20 @@ def tile_networked_sliding_control_s7_kernel(tc, x_bytes, x_scale, c, offset, ga
             for i in range(FPC):
                 k_gain(g, ch * FPC + i)
 
-
-        def turn_unit(i, engines="ss"):
+        def turn_unit(i):
             ch, half = divmod(i, 2)
             for g in (2 * half, 2 * half + 1):
                 k_turn(g, ch)
             for g in (2 * half, 2 * half + 1):
-                k_copy(g, ch, engines[g % 2])
+                k_copy(g, ch)
 
         def gain_unit(i):
             ch, half = divmod(i, 2)
             gains(2 * half, ch)
             gains(2 * half + 1, ch)
 
-        def quant_unit(i):
-            ch, half = divmod(i, 2)
-            k_quant(2 * half, ch)
-            k_quant(2 * half + 1, ch)
-
-
         load_scale()
         load_offset()
-        warm_tanh()
         load_b_half(0, 0)
         load_x(0, 0)
         load_b_half(0, 1)
@@ -343,50 +333,51 @@ def tile_networked_sliding_control_s7_kernel(tc, x_bytes, x_scale, c, offset, ga
         load_b(2)
         load_x(1, 0)
         load_c(0, 0)
-        load_b(3)
         load_c(1, 0)
+        load_b(3)
         load_b(4)
         load_x(1, 1)
         cast_offset()
         spread_scale(0, "v")
         spread_scale(1, "s")
-        turn_offset()
         for q in range(Q):
             for t in range(2):
                 widen_half(0, t, q)
         b_tile(0)
+        turn_offset()
         b_tile(1)
         load_b(5)
-        for r in range(3):
-            if r:
-                widen_pair(r // 2, r % 2)
-            x_pair(r // 2, r % 2)
-            b_tile(r + 2)
-            if r < 2:
-                load_c(r, 1)
+        x_pair(0, 0)
+        widen_pair(0, 1)
+        b_tile(2)
+        load_c(0, 1)
+        x_pair(0, 1)
+        widen_pair(1, 0)
+        x_pair(1, 0)
+        b_tile(3)
+        load_c(1, 1)
+        b_tile(4)
         c_inter(0, 0, "v")
         c_inter(1, 0, "v")
         load_b(6)
-        load_x(2, 0)
-        load_x(2, 1)
+        load_xg(2)
         load_b(7)
         x_quant(0)
-        c_quant(0, 0)
-        c_quant(1, 0)
-        b_tile(5)
+        quant_c(0)
         widen_pair(1, 1)
-        load_x(3, 0)
-        load_x(3, 1)
+        load_xg(3)
         load_gain()
         c_inter(0, 1, "v")
         c_inter(1, 1, "v")
-        surfaces([(0, ft) for ft in range(4)])
+        surfaces([(0, ft) for ft in range(2)])
+        b_tile(5)
+        surfaces([(0, ft) for ft in range(2, 4)])
         x_pair(1, 1)
         b_tile(6)
-        c_quant(0, 1)
-        c_quant(1, 1)
+        quant_c(1)
+        widen(2, 0)
         x_quant(1)
-        widen_pair(2, 0)
+        widen(2, 1)
         widen_pair(2, 1)
         surfaces([(0, ft) for ft in range(4, 8)])
         surfaces([(1, ft) for ft in range(2)])
@@ -396,6 +387,7 @@ def tile_networked_sliding_control_s7_kernel(tc, x_bytes, x_scale, c, offset, ga
         surfaces([(1, ft) for ft in range(2, 4)])
         x_pair(2, 1)
         widen_pair(3, 1)
+
         x_quant(2)
         gains(0, 0)
         surfaces([(1, ft) for ft in range(4, 8)])
@@ -408,37 +400,29 @@ def tile_networked_sliding_control_s7_kernel(tc, x_bytes, x_scale, c, offset, ga
         gains(2, 0)
         surfaces([(2, 4), (2, 5)])
         surfaces([(3, ft) for ft in range(4)])
-        b_quant(0)
-        b_quant(1)
+        quant_b(0)
         gains(1, 1)
         gains(3, 0)
         surfaces([(2, 6), (2, 7)])
         turn_unit(0)
         turn_unit(1)
-        b_quant(2)
-        b_quant(3)
+        quant_b(1)
         gains(2, 1)
         surfaces([(3, ft) for ft in range(4, 8)])
-        quant_unit(0)
-        quant_unit(1)
+        quant_k(0)
         gains(3, 1)
-        for n in range(4, 8):
-            b_quant(n)
+        quant_k(1)
+        quant_b(2)
+        quant_b(3)
         turn_unit(2)
-        quant_unit(2)
-        for h in range(6):
-            ch, half = divmod(h, 2)
-            if h + 4 < 8:
-                gain_unit(h + 4)
-            for pair in (2 * half, 2 * half + 1):
-                second(ch, pair)
-                store(ch, pair)
-            if h + 3 < 8:
-                turn_unit(h + 3)
-                quant_unit(h + 3)
-        for pair in range(3):
-            second(3, pair)
-            store(3, pair, "s")
-        for n in (6, 7):
-            second1(3, n)
-            store1(3, n, "s" if n % 2 else "v")
+        quant_k(2)
+        banks = [(ch, (n, n + 1), 0, FC) for ch in range(CH) for n in range(0, NT, 2)]
+        banks = banks[:-2] + [(CH - 1, (n,), 0, FC) for n in range(NT - 4, NT - 1)] + [(CH - 1, (NT - 1,), first, P) for first in (0, P)]
+        for i, (ch, nodes, first, width) in enumerate(banks):
+            if i % 2 == 0 and i // 2 + 4 < 8:
+                gain_unit(i // 2 + 4)
+            nodes_part(ch, nodes, (0, 1, 2, 3), first, width)
+            store_nodes(ch, nodes, "v" if i >= 14 and i % 2 == 0 else "s", first, width)
+            if i % 2 == 1 and i // 2 + 3 < 8:
+                turn_unit(i // 2 + 3)
+                quant_k(i // 2 + 3)

@@ -24,10 +24,10 @@ CH = 4
 FC = F // CH
 FPC = FC // P
 BANKS = 8
-BUFS = {"braw": 6, "cint": 2, "xw": 6, "xint": 2, "bint": 8, "thmod": 8, "kw": 16, "kint": 4, "xb": 4, "vo": 12}
+BUFS = {"braw": 6, "cint": 2, "xw": 6, "xint": 2, "bint": 8, "thmod": 8, "kw": 12, "kint": 6, "xb": 4, "vo": 12}
 KIB = 1024
 AT_RAW = 0
-AT_KW, AT_KINT = AT_RAW, AT_RAW + 16 * KIB
+AT_KW, AT_KINT = AT_RAW, AT_RAW + 12 * KIB
 AT_XB = AT_RAW + 24 * KIB
 AT_XW = AT_XB + 8 * KIB
 AT_VO = AT_XW
@@ -403,26 +403,34 @@ def tile_networked_sliding_control_s7_kernel(tc, x_bytes, x_scale, c, offset, ga
         quant_b(0)
         gains(1, 1)
         gains(3, 0)
-        surfaces([(2, 6), (2, 7)])
         turn_unit(0)
-        turn_unit(1)
         quant_b(1)
-        gains(2, 1)
-        surfaces([(3, ft) for ft in range(4, 8)])
-        quant_k(0)
-        gains(3, 1)
-        quant_k(1)
+        surfaces([(2, 6), (2, 7), (3, 4), (3, 5)])
         quant_b(2)
+        quant_k(0)
         quant_b(3)
-        turn_unit(2)
-        quant_k(2)
-        banks = [(ch, (n, n + 1), 0, FC) for ch in range(CH) for n in range(0, NT, 2)]
-        banks = banks[:-2] + [(CH - 1, (n,), 0, FC) for n in range(NT - 4, NT - 1)] + [(CH - 1, (NT - 1,), first, P) for first in (0, P)]
-        for i, (ch, nodes, first, width) in enumerate(banks):
-            if i % 2 == 0 and i // 2 + 4 < 8:
-                gain_unit(i // 2 + 4)
-            nodes_part(ch, nodes, (0, 1, 2, 3), first, width)
-            store_nodes(ch, nodes, "v" if i >= 14 and i % 2 == 0 else "s", first, width)
-            if i % 2 == 1 and i // 2 + 3 < 8:
-                turn_unit(i // 2 + 3)
-                quant_k(i // 2 + 3)
+        pairs = [(n, n + 1) for n in range(0, NT, 2)]
+        for ch in range(CH - 1):
+            turn_unit(2 * ch + 1)
+            turn_unit(2 * ch + 2)
+            if ch == 0:
+                surfaces([(3, 6), (3, 7)])
+            gains(2, ch + 1)
+            quant_k(2 * ch + 1)
+            gains(3, ch + 1)
+            if ch + 2 < CH:
+                gain_unit(2 * ch + 4)
+            quant_k(2 * ch + 2)
+            for nodes in pairs:
+                nodes_part(ch, nodes, (0, 1))
+            for i, nodes in enumerate(pairs):
+                if ch == CH - 2 and i == 1:
+                    turn_unit(2 * ch + 3)
+                    quant_k(2 * ch + 3)
+                nodes_part(ch, nodes, (2, 3))
+                store_nodes(ch, nodes)
+        for nodes in pairs[:2]:
+            nodes_part(CH - 1, nodes, (0, 1))
+        for i, nodes in enumerate(pairs[:2] + [(n,) for n in range(NT - 4, NT)]):
+            nodes_part(CH - 1, nodes, (2, 3) if i < 2 else (0, 1, 2, 3))
+            store_nodes(CH - 1, nodes, "v" if i % 2 else "s")

@@ -73,13 +73,13 @@ def tile_networked_sliding_control_s7_kernel(tc, x_bytes, x_scale, c, offset, ga
         def load_x(g, u):
             xbytes = pool.tile([P, 2, K], U8, bufs=BUFS["xb"], name="xbytes", align_bytes=64, offset=AT_XB)
             nc.sync.dma_start(out=xbytes[:], in_=x_view[g, u])
-            x_raw[g, u] = xbytes[:]
+            x_raw[g, u] = xbytes[:].rearrange("p e k -> p (e k)")
 
         def load_xg(g):
             xgroup = pool.tile([P, 2, 2, K], U8, name=f"xbytes_group{g}", align_bytes=64, offset=AT_XB + 4 * KIB * (g % 2))
             nc.sync.dma_start(out=xgroup[:].rearrange("p u e k -> p (u e k)"), in_=x_bytes.rearrange("(g p t) k -> g p (t k)", p=P, t=4)[g])
             for u in range(2):
-                x_raw[g, u] = xgroup[:, u]
+                x_raw[g, u] = xgroup[:, u].rearrange("p e k -> p (e k)")
 
         def load_c(q, h):
             raw = pool.tile([P, 4, 512], BF16, bufs=BUFS["braw"], name="raw", align_bytes=64, offset=AT_RAW)
@@ -98,7 +98,6 @@ def tile_networked_sliding_control_s7_kernel(tc, x_bytes, x_scale, c, offset, ga
 
         ident = const.tile([P, P], F32)
         off_rows = const.tile([P, P], BF16)
-        scale_b = const.tile([P, K], F32)
         gain_b = const.tile([P, M], BF16)
         scale_v = const.tile([P, Q, 4], F32)
         off_f = const.tile([P, P], F32)
@@ -112,13 +111,6 @@ def tile_networked_sliding_control_s7_kernel(tc, x_bytes, x_scale, c, offset, ga
 
         def load_gain():
             nc.sync.dma_start(out=gain_b[:], in_=gain.partition_broadcast(P))
-
-        def spread_scale(q, eng):
-            sp = bank()
-            for m in range(4):
-                nc.tensor.transpose(sp[:, m * P : (m + 1) * P], scale_v[:, q, m : m + 1].to_broadcast([P, P]), ident[:])
-            dst = scale_b[:, 512 * q : 512 * (q + 1)].rearrange("p (n m) -> p n m", m=4)
-            copy(eng, dst, sp[:].rearrange("p (m n) -> p n m", m=4))
 
         def cast_offset():
             nc.scalar.copy(out=off_f[:], in_=off_rows[:])
@@ -141,36 +133,32 @@ def tile_networked_sliding_control_s7_kernel(tc, x_bytes, x_scale, c, offset, ga
         def quant_c(h):
             c_codes[h] = quantise(f"c{h}", c_int[h][:], Q * 512)
 
-        def widen(g, t):
-            xw = pool.tile([P, K], BF16, bufs=BUFS["xw"], name="xw", align_bytes=64, offset=AT_XW)
-            nc.vector.tensor_tensor(out=xw[:], in0=x_raw[g, t // 2][:, t % 2, :].bitcast(FP8), in1=scale_b[:], op=MULT)
-            x_wide[g, t] = xw
-
-        def widen_half(g, t, q):
-            if q == 0:
-                xw = pool.tile([P, K], BF16, bufs=BUFS["xw"], name="xw", align_bytes=64, offset=AT_XW)
-                x_wide[g, t] = xw
-            states = slice(512 * q, 512 * (q + 1))
-            nc.vector.tensor_tensor(
-                out=x_wide[g, t][:, states], in0=x_raw[g, t // 2][:, t % 2, states].bitcast(FP8), in1=scale_b[:, states], op=MULT
-            )
+        def widen(g, u, rows=(0, 2)):
+            if rows[0] == 0:
+                x_wide[g, u] = pool.tile([P, 2 * K], BF16, bufs=BUFS["xw"] // 2, name="xw", align_bytes=64, offset=AT_XW)
+            cols = slice(K * rows[0], K * rows[1])
+            nc.scalar.copy(out=x_wide[g, u][:, cols], in_=x_raw[g, u][:, cols].bitcast(FP8))
 
         def x_turn(g, u, q):
             tp = bank()
             for e in range(2):
-                words = x_wide[g, 2 * u + e][:].bitcast(F32)
+                words = x_wide[g, u][:, K * e : K * (e + 1)].bitcast(F32)
                 for w in range(2):
                     i = 2 * e + w
                     nc.tensor.transpose(tp[:, i * P : (i + 1) * P], words[:, 256 * q + w : 256 * (q + 1) : 2], ident[:])
             x_tp[g, u, q] = tp
 
-        def x_copy(g, u, q, eng="s"):
+        def x_scale_out(g, u, q):
             if (u, q) == (0, 0):
                 xint = pool.tile([P, Q * 512 * 4], BF16, bufs=BUFS["xint"], name="xint", align_bytes=64, offset=AT_XINT)
                 x_int[g] = xint
-            first = 1024 * q + 512 * u
-            dst = x_int[g][:].bitcast(F32)[:, first : first + 512]
-            copy(eng, dst.rearrange("p (r i) -> p r i", i=4), x_tp[g, u, q][:].rearrange("p (i r) -> p r i", i=4))
+            first = 2048 * q + 1024 * u
+            nc.vector.tensor_tensor(
+                out=x_int[g][:, first : first + 1024].rearrange("p (r e w h) -> p r e w h", e=2, w=2, h=2),
+                in0=x_tp[g, u, q][:].bitcast(BF16).rearrange("p (e w r h) -> p r e w h", e=2, w=2, h=2),
+                in1=scale_v[:, q].rearrange("p (r e w h) -> p r e w h", r=1, e=1, h=2).to_broadcast([P, P, 2, 2, 2]),
+                op=MULT,
+            )
 
         def x_quant(g):
             x_codes[g] = quantise(f"x{g}", x_int[g][:], Q * 512)
@@ -285,11 +273,13 @@ def tile_networked_sliding_control_s7_kernel(tc, x_bytes, x_scale, c, offset, ga
         nc.vector.memset(ident[:], 0.0)
         make_identity(nc, ident[:], nomemset=True)
         nc.vector.memset(off_rows[:], 0.0)
-        def x_pair(g, u):
+        def x_turns(g, u):
             for q in range(Q):
                 x_turn(g, u, q)
+
+        def x_scales(g, u):
             for q in range(Q):
-                x_copy(g, u, q)
+                x_scale_out(g, u, q)
 
         def b_tile(n):
             for half in range(2):
@@ -302,10 +292,6 @@ def tile_networked_sliding_control_s7_kernel(tc, x_bytes, x_scale, c, offset, ga
                 sigma(g, ft)
             for g, ft in tiles:
                 tanh(g, ft)
-
-        def widen_pair(g, u):
-            widen(g, 2 * u)
-            widen(g, 2 * u + 1)
 
         def gains(g, ch):
             for i in range(FPC):
@@ -325,87 +311,92 @@ def tile_networked_sliding_control_s7_kernel(tc, x_bytes, x_scale, c, offset, ga
 
         load_scale()
         load_offset()
-        load_b_half(0, 0)
         load_x(0, 0)
-        load_b_half(0, 1)
-        load_b(1)
-        load_x(0, 1)
-        load_b(2)
-        load_x(1, 0)
+        load_b_half(0, 0)
         load_c(0, 0)
+        load_b_half(0, 1)
+        load_x(0, 1)
         load_c(1, 0)
+        load_b(1)
+        load_x(1, 0)
+        load_b(2)
         load_b(3)
-        load_b(4)
         load_x(1, 1)
+        widen(0, 0, (0, 1))
+        widen(0, 0, (1, 2))
         cast_offset()
-        spread_scale(0, "v")
-        spread_scale(1, "s")
-        for q in range(Q):
-            for t in range(2):
-                widen_half(0, t, q)
-        b_tile(0)
-        turn_offset()
-        b_tile(1)
-        load_b(5)
-        x_pair(0, 0)
-        widen_pair(0, 1)
-        b_tile(2)
-        load_c(0, 1)
-        x_pair(0, 1)
-        widen_pair(1, 0)
-        x_pair(1, 0)
-        b_tile(3)
-        load_c(1, 1)
-        b_tile(4)
+        b_turn(0, 0)
+        x_turns(0, 0)
+        b_copy(0, 0)
+        x_scale_out(0, 0, 0)
         c_inter(0, 0, "v")
+        x_scale_out(0, 0, 1)
+        b_turn(0, 1)
+        widen(0, 1)
+        b_copy(0, 1)
+        turn_offset()
+        x_turns(0, 1)
         c_inter(1, 0, "v")
-        load_b(6)
-        load_xg(2)
-        load_b(7)
-        x_quant(0)
+        x_scales(0, 1)
+        load_c(0, 1)
+        load_c(1, 1)
+        b_tile(1)
+        widen(1, 0)
         quant_c(0)
-        widen_pair(1, 1)
-        load_xg(3)
-        load_gain()
+        x_quant(0)
+        load_b(4)
+        b_tile(2)
+        x_turns(1, 0)
+        x_scales(1, 0)
+        load_xg(2)
+        load_b(5)
+        widen(1, 1)
+        b_tile(3)
+        surfaces([(0, ft) for ft in range(4)])
         c_inter(0, 1, "v")
         c_inter(1, 1, "v")
-        surfaces([(0, ft) for ft in range(2)])
-        b_tile(5)
-        surfaces([(0, ft) for ft in range(2, 4)])
-        x_pair(1, 1)
-        b_tile(6)
         quant_c(1)
+        load_b(6)
+        load_b(7)
+        x_turns(1, 1)
         widen(2, 0)
+        b_tile(4)
+        x_scales(1, 1)
         x_quant(1)
-        widen(2, 1)
-        widen_pair(2, 1)
+        load_xg(3)
+        load_gain()
         surfaces([(0, ft) for ft in range(4, 8)])
-        surfaces([(1, ft) for ft in range(2)])
-        b_tile(7)
-        x_pair(2, 0)
-        widen_pair(3, 0)
-        surfaces([(1, ft) for ft in range(2, 4)])
-        x_pair(2, 1)
-        widen_pair(3, 1)
-
-        x_quant(2)
+        x_turns(2, 0)
+        widen(2, 1)
+        b_tile(5)
+        x_scales(2, 0)
+        surfaces([(1, ft) for ft in range(4)])
+        x_turns(2, 1)
+        widen(3, 0)
+        b_tile(6)
         gains(0, 0)
+        x_scales(2, 1)
+        x_quant(2)
         surfaces([(1, ft) for ft in range(4, 8)])
-        x_pair(3, 0)
-        x_pair(3, 1)
-        surfaces([(2, ft) for ft in range(4)])
+        x_turns(3, 0)
+        widen(3, 1)
+        b_tile(7)
         gains(1, 0)
-        gains(0, 1)
+        x_scales(3, 0)
+        surfaces([(2, ft) for ft in range(4)])
+        x_turns(3, 1)
+        quant_b(0)
+        x_scales(3, 1)
         x_quant(3)
         gains(2, 0)
-        surfaces([(2, 4), (2, 5)])
+        surfaces([(2, ft) for ft in range(4,8)])
         surfaces([(3, ft) for ft in range(4)])
-        quant_b(0)
-        gains(1, 1)
-        gains(3, 0)
-        turn_unit(0)
         quant_b(1)
-        surfaces([(2, 6), (2, 7), (3, 4), (3, 5)])
+        gains(0, 1)
+        gains(3, 0)
+        gains(1, 1)
+        turn_unit(0)
+        surfaces([(3, 4), (3, 5)])
         quant_b(2)
         quant_k(0)
         quant_b(3)

@@ -35,6 +35,7 @@ AT_XINT = AT_XW + 12 * KIB
 AT_BINT = AT_XINT + 16 * KIB
 AT_TH = AT_BINT + 32 * KIB
 AT_CINT = AT_TH + 56 * KIB
+AT_SORT = AT_TH + 44 * KIB
 
 
 def tile_networked_sliding_control_s7_kernel(tc, x_bytes, x_scale, c, offset, gain, bmat, out):
@@ -48,7 +49,7 @@ def tile_networked_sliding_control_s7_kernel(tc, x_bytes, x_scale, c, offset, ga
         x_view = x_bytes.rearrange("(g p u e) k -> g u p e k", p=P, u=2, e=2)
         c_view = c.rearrange("(q p j) (h f) -> q h p j f", p=P, j=4, h=2)
         b_view = bmat.rearrange("(n p) m -> n p m", p=P)
-        x_raw, c_raw, b_raw = {}, {}, {}
+        x_raw, c_raw, b_raw, b_whole, b_sorted, x_sorted, x_cast = {}, {}, {}, {}, {}, {}, {}
         banks_taken, kept_widths = [], []
 
         def bank():
@@ -56,40 +57,57 @@ def tile_networked_sliding_control_s7_kernel(tc, x_bytes, x_scale, c, offset, ga
             banks_taken.append(tile)
             return tile
 
+        ring_count = {}
+
+        def ring(name, shape, dtype, slots, at, size):
+            i = ring_count.get(name, 0)
+            ring_count[name] = i + 1
+            return pool.tile(shape, dtype, name=f"{name}{i}", align_bytes=64, offset=at + size * (i % slots))
+
         def copy(eng, dst, src):
             if eng == "v":
                 nc.vector.tensor_copy(out=dst, in_=src)
             else:
                 nc.scalar.copy(out=dst, in_=src)
 
-        def quantise(name, src, width):
+        def code_tiles(name, width):
             first = 5 * sum(kept_widths)
             kept_widths.append(width)
             codes = kept.tile([P, width], U32, name=f"codes_{name}", align_bytes=256, offset=first)
             scales = kept.tile([P, width], U8, name=f"scales_{name}", align_bytes=256, offset=first + 4 * width)
-            nc.vector.quantize_mx(out=codes[:].bitcast(FP8X4), scales=scales[:], in_=src)
             return codes, scales
 
+        def quantise_into(tiles, src, first, width):
+            codes, scales = tiles
+            words = slice(first, first + width)
+            nc.vector.quantize_mx(out=codes[:, words].bitcast(FP8X4), scales=scales[:, words], in_=src[:, 4 * first : 4 * (first + width)])
+
+        def quantise(name, src, width):
+            tiles = code_tiles(name, width)
+            quantise_into(tiles, src, 0, width)
+            return tiles
+
         def load_x(g, u):
-            xbytes = pool.tile([P, 2, K], U8, bufs=BUFS["xb"], name="xbytes", align_bytes=64, offset=AT_XB)
+            xbytes = ring("xbytes", [P, 2, K], U8, BUFS["xb"], AT_XB, 2 * KIB)
             nc.sync.dma_start(out=xbytes[:], in_=x_view[g, u])
-            x_raw[g, u] = xbytes[:].rearrange("p e k -> p (e k)")
+            x_raw[g, u] = xbytes[:]
 
         def load_xg(g):
             xgroup = pool.tile([P, 2, 2, K], U8, name=f"xbytes_group{g}", align_bytes=64, offset=AT_XB + 4 * KIB * (g % 2))
             nc.sync.dma_start(out=xgroup[:].rearrange("p u e k -> p (u e k)"), in_=x_bytes.rearrange("(g p t) k -> g p (t k)", p=P, t=4)[g])
             for u in range(2):
-                x_raw[g, u] = xgroup[:, u].rearrange("p e k -> p (e k)")
+                x_raw[g, u] = xgroup[:, u]
 
         def load_c(q, h):
-            raw = pool.tile([P, 4, 512], BF16, bufs=BUFS["braw"], name="raw", align_bytes=64, offset=AT_RAW)
+            raw = ring("raw", [P, 4, 512], BF16, BUFS["braw"], AT_RAW, 4 * KIB)
             nc.sync.dma_start(out=raw[:], in_=c_view[q, h])
             c_raw[q, h] = raw
 
         def load_b(n):
-            raw = pool.tile([P, M], BF16, bufs=BUFS["braw"], name="raw", align_bytes=64, offset=AT_RAW)
+            raw = ring("raw", [P, M], BF16, BUFS["braw"], AT_RAW, 4 * KIB)
             nc.sync.dma_start(out=raw[:], in_=b_view[n])
             b_raw[n] = [raw[:, 0 : M // 2], raw[:, M // 2 : M]]
+            b_whole[n] = raw
 
         def load_b_half(n, half):
             raw = pool.tile([P, M // 2], BF16, name=f"raw_half{half}", align_bytes=64, offset=AT_TH + 2 * KIB * half)
@@ -98,6 +116,7 @@ def tile_networked_sliding_control_s7_kernel(tc, x_bytes, x_scale, c, offset, ga
 
         ident = const.tile([P, P], F32)
         off_rows = const.tile([P, P], BF16)
+        scale_b = const.tile([P, K], F32)
         gain_b = const.tile([P, M], BF16)
         scale_v = const.tile([P, Q, 4], F32)
         off_f = const.tile([P, P], F32)
@@ -109,8 +128,16 @@ def tile_networked_sliding_control_s7_kernel(tc, x_bytes, x_scale, c, offset, ga
         def load_offset():
             nc.scalar.dma_start(out=off_rows[0:FT, :], in_=offset.rearrange("(c p) -> c p", p=P))
 
-        def load_gain():
-            nc.sync.dma_start(out=gain_b[:], in_=gain.partition_broadcast(P))
+        def load_gain(half):
+            cols = slice(M // 2 * half, M // 2 * (half + 1))
+            nc.sync.dma_start(out=gain_b[:, cols], in_=gain[cols].partition_broadcast(P))
+
+        def spread_scale(q, eng):
+            sp = bank()
+            for m in range(4):
+                nc.tensor.transpose(sp[:, m * P : (m + 1) * P], scale_v[:, q, m : m + 1].to_broadcast([P, P]), ident[:])
+            dst = scale_b[:, 512 * q : 512 * (q + 1)].rearrange("p (n m) -> p n m", m=4)
+            copy(eng, dst, sp[:].rearrange("p (m n) -> p n m", m=4))
 
         def cast_offset():
             nc.scalar.copy(out=off_f[:], in_=off_rows[:])
@@ -131,27 +158,32 @@ def tile_networked_sliding_control_s7_kernel(tc, x_bytes, x_scale, c, offset, ga
             copy(eng, dst, c_raw[q, h][:].rearrange("p t (c i) -> p c t i", i=4))
 
         def quant_c(h):
-            c_codes[h] = quantise(f"c{h}", c_int[h][:], Q * 512)
+            c_codes[h] = quantise(f"c{h}", c_int[h], Q * 512)
 
-        def widen(g, u, rows=(0, 2)):
-            if rows[0] == 0:
-                x_wide[g, u] = pool.tile([P, 2 * K], BF16, bufs=BUFS["xw"] // 2, name="xw", align_bytes=64, offset=AT_XW)
-            cols = slice(K * rows[0], K * rows[1])
-            nc.scalar.copy(out=x_wide[g, u][:, cols], in_=x_raw[g, u][:, cols].bitcast(FP8))
+        def widen(g, t):
+            xw = ring("xw", [P, K], BF16, BUFS["xw"], AT_XW, 2 * KIB)
+            nc.vector.tensor_tensor(out=xw[:], in0=x_raw[g, t // 2][:, t % 2, :].bitcast(FP8), in1=scale_b[:], op=MULT)
+            x_wide[g, t] = xw
 
-        def x_turn(g, u, q):
-            tp = bank()
+        def widen_half(g, t, q):
+            if q == 0:
+                xw = ring("xw", [P, K], BF16, BUFS["xw"], AT_XW, 2 * KIB)
+                x_wide[g, t] = xw
+            states = slice(512 * q, 512 * (q + 1))
+            nc.vector.tensor_tensor(
+                out=x_wide[g, t][:, states], in0=x_raw[g, t // 2][:, t % 2, states].bitcast(FP8), in1=scale_b[:, states], op=MULT
+            )
+
+        def cast_pair(g, u):
+            xw = ring("xc", [P, 2, K], BF16, 2, AT_XW + 4 * KIB, 4 * KIB)
+            nc.scalar.copy(out=xw[:].rearrange("p e k -> p (e k)"), in_=x_raw[g, u].rearrange("p e k -> p (e k)").bitcast(FP8))
+            x_cast[g, u] = xw
             for e in range(2):
-                words = x_wide[g, u][:, K * e : K * (e + 1)].bitcast(F32)
-                for w in range(2):
-                    i = 2 * e + w
-                    nc.tensor.transpose(tp[:, i * P : (i + 1) * P], words[:, 256 * q + w : 256 * (q + 1) : 2], ident[:])
-            x_tp[g, u, q] = tp
+                x_wide[g, 2 * u + e] = xw[:, e]
 
         def x_scale_out(g, u, q):
             if (u, q) == (0, 0):
-                xint = pool.tile([P, Q * 512 * 4], BF16, bufs=BUFS["xint"], name="xint", align_bytes=64, offset=AT_XINT)
-                x_int[g] = xint
+                x_int[g] = pool.tile([P, Q * 512 * 4], BF16, name=f"xscaled{g}", align_bytes=64, offset=(AT_XINT, AT_CINT)[g % 2])
             first = 2048 * q + 1024 * u
             nc.vector.tensor_tensor(
                 out=x_int[g][:, first : first + 1024].rearrange("p (r e w h) -> p r e w h", e=2, w=2, h=2),
@@ -160,28 +192,68 @@ def tile_networked_sliding_control_s7_kernel(tc, x_bytes, x_scale, c, offset, ga
                 op=MULT,
             )
 
+        def sort_words(dst, src):
+            nc.vector.tensor_copy(out=dst.rearrange("p (g w r) -> p g w r", w=2, r=P), in_=src.rearrange("p (g r w) -> p g w r", w=2, r=P))
+
+        def b_sort(n):
+            b_sorted[n] = ring("sorted", [P, M // 2], F32, 3, AT_SORT, 4 * KIB)
+            sort_words(b_sorted[n][:], b_whole[n][:].bitcast(F32))
+
+        def x_sort(g, u):
+            x_sorted[g, u] = ring("sorted", [P, K], F32, 3, AT_SORT, 4 * KIB)
+            sort_words(x_sorted[g, u][:], x_cast[g, u][:].rearrange("p e k -> p (e k)").bitcast(F32))
+
+        def x_turn(g, u, q):
+            tp = bank()
+            for e in range(2):
+                for w in range(2):
+                    i = 2 * e + w
+                    if (g, u) in x_sorted:
+                        words = x_sorted[g, u][:, 512 * e + 256 * q + P * w : 512 * e + 256 * q + P * (w + 1)]
+                    else:
+                        words = x_wide[g, 2 * u + e][:].bitcast(F32)[:, 256 * q + w : 256 * (q + 1) : 2]
+                    nc.tensor.transpose(tp[:, i * P : (i + 1) * P], words, ident[:])
+            x_tp[g, u, q] = tp
+
+        def x_copy(g, u, q, eng="s"):
+            if (u, q) == (0, 0):
+                xint = ring("xint", [P, Q * 512 * 4], BF16, BUFS["xint"], AT_XINT, 8 * KIB)
+                x_int[g] = xint
+            first = 1024 * q + 512 * u
+            dst = x_int[g][:].bitcast(F32)[:, first : first + 512]
+            copy(eng, dst.rearrange("p (r i) -> p r i", i=4), x_tp[g, u, q][:].rearrange("p (i r) -> p r i", i=4))
+
         def x_quant(g):
-            x_codes[g] = quantise(f"x{g}", x_int[g][:], Q * 512)
+            x_codes[g] = quantise(f"x{g}", x_int[g], Q * 512)
+
+        def x_quant_pair(g, u):
+            if u == 0:
+                x_codes[g] = code_tiles(f"x{g}", Q * 512)
+            for q in range(Q):
+                quantise_into(x_codes[g], x_int[g], 512 * q + 256 * u, 256)
 
         def b_turn(n, half):
-            words = b_raw[n][half].bitcast(F32)
             tp = bank()
             for gl in range(2):
                 for w in range(2):
                     i = 2 * gl + w
-                    nc.tensor.transpose(tp[:, i * P : (i + 1) * P], words[:, 256 * gl + w : 256 * (gl + 1) : 2], ident[:])
+                    if n in b_sorted:
+                        words = b_sorted[n][:, 512 * half + P * i : 512 * half + P * (i + 1)]
+                    else:
+                        words = b_raw[n][half].bitcast(F32)[:, 256 * gl + w : 256 * (gl + 1) : 2]
+                    nc.tensor.transpose(tp[:, i * P : (i + 1) * P], words, ident[:])
             b_tp[n, half] = tp
 
         def b_copy(n, half, eng="s"):
             if n % 2 == 0 and half == 0:
-                bint = pool.tile([P, 2 * G * P * 4], BF16, bufs=NT // 2, name="bint", align_bytes=64, offset=AT_BINT)
+                bint = ring("bint", [P, 2 * G * P * 4], BF16, NT // 2, AT_BINT, 8 * KIB)
                 b_int[n // 2] = bint
             first = 1024 * (n % 2) + 512 * half
             dst = b_int[n // 2][:].bitcast(F32)[:, first : first + 512]
             copy(eng, dst.rearrange("p (g r w) -> p g r w", g=2, w=2), b_tp[n, half][:].rearrange("p (g w r) -> p g r w", g=2, w=2))
 
         def quant_b(pair):
-            b_codes[pair] = quantise(f"b{pair}", b_int[pair][:], 2 * G * P)
+            b_codes[pair] = quantise(f"b{pair}", b_int[pair], 2 * G * P)
 
         s_ps, tanh_t, k_wide, k_tp, k_int, v_ps = {}, {}, {}, {}, {}, {}
 
@@ -203,14 +275,45 @@ def tile_networked_sliding_control_s7_kernel(tc, x_bytes, x_scale, c, offset, ga
                 )
             s_ps[g, ft] = ps
 
-        def tanh(g, ft):
-            th = pool.tile([P, 512], F32, name=f"th{g}{ft}", align_bytes=64, offset=AT_TH + 2 * KIB * len(tanh_t))
-            nc.scalar.activation(out=th[:], in_=s_ps[g, ft][:], func=ACT.Tanh, bias=off_cols[:, ft : ft + 1])
-            tanh_t[g, ft] = th
+        def tanh_tile(g, ft):
+            if (g, ft) not in tanh_t:
+                tanh_t[g, ft] = pool.tile([P, 512], F32, name=f"th{g}{ft}", align_bytes=64, offset=AT_TH + 2 * KIB * len(tanh_t))
+            return tanh_t[g, ft]
 
-        def k_gain(g, ft):
-            kw = pool.tile([P, 512], BF16, bufs=BUFS["kw"], name="kw", align_bytes=64, offset=AT_KW)
-            nc.vector.tensor_tensor(
+        def tanh(g, ft):
+            nc.scalar.activation(out=tanh_tile(g, ft)[:], in_=s_ps[g, ft][:], func=ACT.Tanh, bias=off_cols[:, ft : ft + 1])
+
+        def sigma_pair(g, u, fts):
+            ps = bank()
+            xc, xs = x_codes[g]
+            for i, ft in enumerate(fts):
+                cc, cs = c_codes[ft // 4]
+                for q in range(Q):
+                    col = slice(512 * q + (ft % 4) * P, 512 * q + (ft % 4 + 1) * P)
+                    agents = slice(512 * q + 256 * u, 512 * q + 256 * (u + 1))
+                    nc.tensor.matmul_mx(
+                        out=ps[:, 256 * i : 256 * (i + 1)],
+                        lhsT=cc[:, col].bitcast(FP8X4),
+                        lhsT_scale=cs[:, col],
+                        rhs=xc[:, agents].bitcast(FP8X4),
+                        rhs_scale=xs[:, agents],
+                        start=(q == 0),
+                        stop=(q == Q - 1),
+                    )
+            s_ps[g, u, fts] = ps
+
+        def tanh_pair(g, u, fts):
+            for i, ft in enumerate(fts):
+                nc.scalar.activation(
+                    out=tanh_tile(g, ft)[:, 256 * u : 256 * (u + 1)], in_=s_ps[g, u, fts][:, 256 * i : 256 * (i + 1)], func=ACT.Tanh, bias=off_cols[:, ft : ft + 1]
+                )
+
+        def k_gain(g, ft, at=None):
+            if at is None:
+                kw = ring("kw", [P, 512], BF16, BUFS["kw"], AT_KW, KIB)
+            else:
+                kw = pool.tile([P, 512], BF16, name=f"kw_pool{g}{ft}", align_bytes=64, offset=at)
+            (nc.vector if at is None else nc.gpsimd).tensor_tensor(
                 out=kw[:].rearrange("f (u p e) -> f u p e", u=2, e=2),
                 in0=tanh_t[g, ft][:].rearrange("f (u p e) -> f u p e", u=2, e=2),
                 in1=gain_b[:, 512 * g : 512 * (g + 1)].rearrange("f (p u e) -> f u p e", u=2, e=2),
@@ -229,14 +332,14 @@ def tile_networked_sliding_control_s7_kernel(tc, x_bytes, x_scale, c, offset, ga
 
         def k_copy(g, ch, eng="s"):
             if g % 2 == 0:
-                kint = pool.tile([P, 2 * FC * 4], BF16, bufs=BUFS["kint"] // 2, name="kint", align_bytes=64, offset=AT_KINT)
+                kint = ring("kint", [P, 2 * FC * 4], BF16, BUFS["kint"] // 2, AT_KINT, 4 * KIB)
                 k_int[g // 2, ch] = kint
             dst = k_int[g // 2, ch][:].bitcast(F32)[:, 512 * (g % 2) : 512 * (g % 2 + 1)]
             copy(eng, dst.rearrange("p (i f u) -> p i f u", i=FPC, u=2), k_tp[g, ch][:].rearrange("p (i u f) -> p i f u", i=FPC, u=2))
 
         def quant_k(unit):
             ch, half = divmod(unit, 2)
-            k_codes[half, ch] = quantise(f"k{unit}", k_int[half, ch][:], 2 * FC)
+            k_codes[half, ch] = quantise(f"k{unit}", k_int[half, ch], 2 * FC)
 
         def nodes_part(ch, nodes, groups, first=0, width=FC):
             if groups[0] == 0:
@@ -259,7 +362,7 @@ def tile_networked_sliding_control_s7_kernel(tc, x_bytes, x_scale, c, offset, ga
                     )
 
         def store_nodes(ch, nodes, eng="s", first=0, width=FC):
-            vo = pool.tile([P, 2 * FC], F32, bufs=BUFS["vo"], name="vo", align_bytes=64, offset=AT_VO)
+            vo = ring("vo", [P, 2 * FC], F32, BUFS["vo"], AT_VO, 2 * KIB)
             used = width * len(nodes)
             copy(eng, vo[:, 0:used], v_ps[ch, nodes, first][:, 0:used])
             rows = slice(nodes[0] * P, (nodes[-1] + 1) * P)
@@ -277,15 +380,29 @@ def tile_networked_sliding_control_s7_kernel(tc, x_bytes, x_scale, c, offset, ga
             for q in range(Q):
                 x_turn(g, u, q)
 
+        def x_copies(g, u, eng="s"):
+            for q in range(Q):
+                x_copy(g, u, q, eng)
+
         def x_scales(g, u):
             for q in range(Q):
                 x_scale_out(g, u, q)
 
-        def b_tile(n):
+        def x_pair(g, u):
+            x_turns(g, u)
+            x_copies(g, u)
+
+        def b_turns(n):
             for half in range(2):
                 b_turn(n, half)
+
+        def b_copies(n, eng="s"):
             for half in range(2):
-                b_copy(n, half)
+                b_copy(n, half, eng)
+
+        def b_tile(n):
+            b_turns(n)
+            b_copies(n)
 
         def surfaces(tiles):
             for g, ft in tiles:
@@ -293,16 +410,34 @@ def tile_networked_sliding_control_s7_kernel(tc, x_bytes, x_scale, c, offset, ga
             for g, ft in tiles:
                 tanh(g, ft)
 
+        def surfaces_pair(g, u, h):
+            halves = [(4 * h, 4 * h + 1), (4 * h + 2, 4 * h + 3)]
+            for fts in halves:
+                sigma_pair(g, u, fts)
+            for fts in halves:
+                tanh_pair(g, u, fts)
+
+        def widen_pair(g, u):
+            widen(g, 2 * u)
+            widen(g, 2 * u + 1)
+
         def gains(g, ch):
             for i in range(FPC):
                 k_gain(g, ch * FPC + i)
 
-        def turn_unit(i):
+        def unit_turns(i):
             ch, half = divmod(i, 2)
             for g in (2 * half, 2 * half + 1):
                 k_turn(g, ch)
+
+        def unit_copies(i, eng="s"):
+            ch, half = divmod(i, 2)
             for g in (2 * half, 2 * half + 1):
-                k_copy(g, ch)
+                k_copy(g, ch, eng)
+
+        def turn_unit(i):
+            unit_turns(i)
+            unit_copies(i)
 
         def gain_unit(i):
             ch, half = divmod(i, 2)
@@ -311,101 +446,111 @@ def tile_networked_sliding_control_s7_kernel(tc, x_bytes, x_scale, c, offset, ga
 
         load_scale()
         load_offset()
-        load_x(0, 0)
         load_b_half(0, 0)
-        load_c(0, 0)
+        load_x(0, 0)
         load_b_half(0, 1)
-        load_x(0, 1)
-        load_c(1, 0)
         load_b(1)
-        load_x(1, 0)
+        load_x(0, 1)
         load_b(2)
+        load_x(1, 0)
+        load_c(0, 0)
+        load_c(1, 0)
         load_b(3)
-        load_x(1, 1)
-        widen(0, 0, (0, 1))
-        widen(0, 0, (1, 2))
-        cast_offset()
-        b_turn(0, 0)
-        x_turns(0, 0)
-        b_copy(0, 0)
-        x_scale_out(0, 0, 0)
-        c_inter(0, 0, "v")
-        x_scale_out(0, 0, 1)
-        b_turn(0, 1)
-        widen(0, 1)
-        b_copy(0, 1)
-        turn_offset()
-        x_turns(0, 1)
-        c_inter(1, 0, "v")
-        x_scales(0, 1)
-        load_c(0, 1)
-        load_c(1, 1)
-        b_tile(1)
-        widen(1, 0)
-        quant_c(0)
-        x_quant(0)
         load_b(4)
-        b_tile(2)
-        x_turns(1, 0)
-        x_scales(1, 0)
+        load_x(1, 1)
+        cast_offset()
+        spread_scale(0, "v")
+        spread_scale(1, "s")
+        for q in range(Q):
+            for t in range(2):
+                widen_half(0, t, q)
+        b_tile(0)
+        turn_offset()
+        b_tile(1)
+        x_pair(0, 0)
+        widen_pair(0, 1)
         load_xg(2)
-        load_b(5)
-        widen(1, 1)
+        load_c(0, 1)
+        b_tile(2)
+        load_c(1, 1)
+        x_pair(0, 1)
+        widen_pair(1, 0)
+        x_pair(1, 0)
         b_tile(3)
-        surfaces([(0, ft) for ft in range(4)])
+        b_tile(4)
+        c_inter(0, 0, "v")
+        load_b(5)
+        load_gain(0)
+        c_inter(1, 0, "v")
+        load_b(6)
+        x_quant(0)
+        quant_c(0)
+        widen_pair(1, 1)
+        load_xg(3)
+        load_b(7)
+        load_gain(1)
+        cast_pair(2, 0)
         c_inter(0, 1, "v")
         c_inter(1, 1, "v")
-        quant_c(1)
-        load_b(6)
-        load_b(7)
-        x_turns(1, 1)
-        widen(2, 0)
-        b_tile(4)
-        x_scales(1, 1)
-        x_quant(1)
-        load_xg(3)
-        load_gain()
-        surfaces([(0, ft) for ft in range(4, 8)])
+        surfaces([(0, 0), (0, 1)])
+        x_pair(1, 1)
+        cast_pair(2, 1)
+        surfaces([(0, 2), (0, 3)])
         x_turns(2, 0)
-        widen(2, 1)
         b_tile(5)
+        quant_c(1)
+        x_quant(1)
+        for i in range(3):
+            k_gain(0, i, AT_XINT + 8 * KIB + KIB * i)
         x_scales(2, 0)
-        surfaces([(1, ft) for ft in range(4)])
+        surfaces([(0, 4), (0, 5)])
         x_turns(2, 1)
-        widen(3, 0)
-        b_tile(6)
-        gains(0, 0)
+        cast_pair(3, 0)
         x_scales(2, 1)
+        surfaces([(0, 6), (0, 7)])
+        cast_pair(3, 1)
+        surfaces([(1, ft) for ft in range(4)])
+        b_sort(6)
         x_quant(2)
-        surfaces([(1, ft) for ft in range(4, 8)])
+        x_sort(3, 0)
+        x_sort(3, 1)
+        for i, (g, ft) in enumerate([(1, 0), (1, 1), (0, 3)]):
+            k_gain(g, ft, AT_XW + 8 * KIB + KIB * i)
+        surfaces([(1, 4), (1, 5)])
+        b_tile(6)
         x_turns(3, 0)
-        widen(3, 1)
-        b_tile(7)
-        gains(1, 0)
-        x_scales(3, 0)
-        surfaces([(2, ft) for ft in range(4)])
         x_turns(3, 1)
-        quant_b(0)
+        x_scales(3, 0)
         x_scales(3, 1)
+        b_sort(7)
         x_quant(3)
-        gains(2, 0)
-        surfaces([(2, ft) for ft in range(4,8)])
-        surfaces([(3, ft) for ft in range(4)])
-        quant_b(1)
-        gains(0, 1)
-        gains(3, 0)
-        gains(1, 1)
+        surfaces([(2, ft) for ft in range(4)])
+        surfaces([(1, 6), (1, 7), (2, 4), (2, 5)])
+        b_tile(7)
         turn_unit(0)
-        surfaces([(3, 4), (3, 5)])
+        quant_b(0)
+        gains(2, 0)
+        quant_b(1)
+        surfaces([(3, ft) for ft in range(4)])
+        gains(1, 1)
+        gains(3, 0)
         quant_b(2)
         quant_k(0)
         quant_b(3)
+        surfaces([(2, 6), (2, 7), (3, 4), (3, 5)])
+        sigma(3, 6)
+        sigma(3, 7)
+        unit_turns(1)
+        unit_turns(2)
+        unit_copies(1)
+        tanh(3, 6)
+        tanh(3, 7)
+        unit_copies(2)
         pairs = [(n, n + 1) for n in range(0, NT, 2)]
         for ch in range(CH - 1):
-            turn_unit(2 * ch + 1)
-            turn_unit(2 * ch + 2)
-            if ch == 0:
-                surfaces([(3, 6), (3, 7)])
+            if ch > 0:
+                turn_unit(2 * ch + 1)
+                turn_unit(2 * ch + 2)
             gains(2, ch + 1)
             quant_k(2 * ch + 1)
             gains(3, ch + 1)

@@ -24,6 +24,7 @@ CH = 4
 FC = F // CH
 FPC = FC // P
 BANKS = 8
+KW_SLOTS = 12
 BUFS = {"braw": 6, "cint": 2, "xw": 6, "xint": 2, "bint": 8, "thmod": 8, "kw": 12, "kint": 6, "xb": 4, "vo": 12}
 KIB = 1024
 AT_RAW = 0
@@ -35,7 +36,7 @@ AT_XINT = AT_XW + 12 * KIB
 AT_BINT = AT_XINT + 16 * KIB
 AT_TH = AT_BINT + 32 * KIB
 AT_CINT = AT_TH + 56 * KIB
-AT_SORT = AT_TH + 44 * KIB
+AT_SORT = AT_TH + 40 * KIB
 
 
 def tile_networked_sliding_control_s7_kernel(tc, x_bytes, x_scale, c, offset, gain, bmat, out):
@@ -63,6 +64,9 @@ def tile_networked_sliding_control_s7_kernel(tc, x_bytes, x_scale, c, offset, ga
             i = ring_count.get(name, 0)
             ring_count[name] = i + 1
             return pool.tile(shape, dtype, name=f"{name}{i}", align_bytes=64, offset=at + size * (i % slots))
+
+        def pass_banks(count):
+            banks_taken.extend([None] * count)
 
         def copy(eng, dst, src):
             if eng == "v":
@@ -117,7 +121,11 @@ def tile_networked_sliding_control_s7_kernel(tc, x_bytes, x_scale, c, offset, ga
         ident = const.tile([P, P], F32)
         off_rows = const.tile([P, P], BF16)
         scale_b = const.tile([P, K], F32)
-        gain_b = const.tile([P, M], BF16)
+        gain_b = const.tile([P, M // 2], BF16)
+        ones = const.tile([P, P], BF16)
+        gain_raw = pool.tile([1, M // 2], BF16, name="gain_raw", align_bytes=64, offset=AT_TH + 12 * KIB)
+        gain_row = pool.tile([P, M // 2], BF16, name="gain_row", align_bytes=64, offset=AT_TH + 8 * KIB)
+        gain_s = const.tile([P, M // 2], BF16)
         scale_v = const.tile([P, Q, 4], F32)
         off_f = const.tile([P, P], F32)
         off_cols = const.tile([P, FT], F32)
@@ -128,9 +136,8 @@ def tile_networked_sliding_control_s7_kernel(tc, x_bytes, x_scale, c, offset, ga
         def load_offset():
             nc.scalar.dma_start(out=off_rows[0:FT, :], in_=offset.rearrange("(c p) -> c p", p=P))
 
-        def load_gain(half):
-            cols = slice(M // 2 * half, M // 2 * (half + 1))
-            nc.sync.dma_start(out=gain_b[:, cols], in_=gain[cols].partition_broadcast(P))
+        def load_gain():
+            nc.sync.dma_start(out=gain_b[:], in_=gain[M // 2 : M].partition_broadcast(P))
 
         def spread_scale(q, eng):
             sp = bank()
@@ -276,12 +283,13 @@ def tile_networked_sliding_control_s7_kernel(tc, x_bytes, x_scale, c, offset, ga
             s_ps[g, ft] = ps
 
         def tanh_tile(g, ft):
-            if (g, ft) not in tanh_t:
-                tanh_t[g, ft] = pool.tile([P, 512], F32, name=f"th{g}{ft}", align_bytes=64, offset=AT_TH + 2 * KIB * len(tanh_t))
-            return tanh_t[g, ft]
+            h, i = divmod(ft, 4)
+            if (g, h) not in tanh_t:
+                tanh_t[g, h] = pool.tile([P, 4, 512], F32, name=f"th{g}{h}", align_bytes=64, offset=AT_TH + 8 * KIB * len(tanh_t))
+            return tanh_t[g, h][:, i]
 
         def tanh(g, ft):
-            nc.scalar.activation(out=tanh_tile(g, ft)[:], in_=s_ps[g, ft][:], func=ACT.Tanh, bias=off_cols[:, ft : ft + 1])
+            nc.scalar.activation(out=tanh_tile(g, ft), in_=s_ps[g, ft][:], func=ACT.Tanh, bias=off_cols[:, ft : ft + 1])
 
         def sigma_pair(g, u, fts):
             ps = bank()
@@ -308,23 +316,48 @@ def tile_networked_sliding_control_s7_kernel(tc, x_bytes, x_scale, c, offset, ga
                     out=tanh_tile(g, ft)[:, 256 * u : 256 * (u + 1)], in_=s_ps[g, u, fts][:, 256 * i : 256 * (i + 1)], func=ACT.Tanh, bias=off_cols[:, ft : ft + 1]
                 )
 
-        def k_gain(g, ft, at=None):
+        kw_taken = []
+
+        def kw_place(count):
+            first = len(kw_taken) % KW_SLOTS
+            kw_taken.extend([None] * count)
+            return AT_KW + KIB * first
+
+        def load_gain_row():
+            nc.sync.dma_start(out=gain_raw[:], in_=gain[0 : M // 2].rearrange("(o m) -> o m", o=1))
+
+        def sort_gain_row():
+            nc.scalar.copy(
+                out=gain_row[0:1, :].bitcast(F32).rearrange("p (g w r) -> p g w r", w=2, r=P),
+                in_=gain_raw[:].bitcast(F32).rearrange("p (g r w) -> p g w r", w=2, r=P),
+            )
+
+        def spread_gain():
+            flat = bank()[:].bitcast(BF16)
+            for g in range(2):
+                rows = gain_row[:, 512 * g : 512 * (g + 1)]
+                nc.tensor.matmul(out=flat[:, 512 * g : 512 * (g + 1)], lhsT=ones[:], rhs=rows, start=True, stop=True)
+            nc.scalar.copy(out=gain_s[:], in_=flat)
+
+        def k_gain(g, first, count, at=None):
             if at is None:
-                kw = ring("kw", [P, 512], BF16, BUFS["kw"], AT_KW, KIB)
+                kw = pool.tile([P, count, 512], BF16, name=f"kw{g}{first}", align_bytes=64, offset=kw_place(count))
             else:
-                kw = pool.tile([P, 512], BF16, name=f"kw_pool{g}{ft}", align_bytes=64, offset=at)
+                kw = pool.tile([P, count, 512], BF16, name=f"kw_pool{g}", align_bytes=64, offset=at)
+            h, i = divmod(first, 4)
             (nc.vector if at is None else nc.gpsimd).tensor_tensor(
-                out=kw[:].rearrange("f (u p e) -> f u p e", u=2, e=2),
-                in0=tanh_t[g, ft][:].rearrange("f (u p e) -> f u p e", u=2, e=2),
-                in1=gain_b[:, 512 * g : 512 * (g + 1)].rearrange("f (p u e) -> f u p e", u=2, e=2),
+                out=kw[:],
+                in0=tanh_t[g, h][:, i : i + count],
+                in1=gain_s[:, 512 * g : 512 * (g + 1)].rearrange("f (o a) -> f o a", o=1).to_broadcast([P, count, 512]),
                 op=MULT,
             )
-            k_wide[g, ft] = kw
+            for j in range(count):
+                k_wide[g, first + j] = kw[:, j]
 
         def k_turn(g, ch):
             tp = bank()
             for i in range(FPC):
-                words = k_wide[g, ch * FPC + i][:].bitcast(F32)
+                words = k_wide[g, ch * FPC + i].bitcast(F32)
                 for u in range(2):
                     j = 2 * i + u
                     nc.tensor.transpose(tp[:, j * P : (j + 1) * P], words[:, P * u : P * (u + 1)], ident[:])
@@ -376,6 +409,8 @@ def tile_networked_sliding_control_s7_kernel(tc, x_bytes, x_scale, c, offset, ga
         nc.vector.memset(ident[:], 0.0)
         make_identity(nc, ident[:], nomemset=True)
         nc.vector.memset(off_rows[:], 0.0)
+        nc.vector.memset(ones[:], 1.0)
+        nc.gpsimd.memset(gain_row[:].bitcast(U32), 0)
         def x_turns(g, u):
             for q in range(Q):
                 x_turn(g, u, q)
@@ -421,9 +456,22 @@ def tile_networked_sliding_control_s7_kernel(tc, x_bytes, x_scale, c, offset, ga
             widen(g, 2 * u)
             widen(g, 2 * u + 1)
 
+        def k_gain_unsorted(g, ft):
+            kw = pool.tile([P, 512], BF16, name=f"kw{g}{ft}", align_bytes=64, offset=kw_place(1))
+            nc.vector.tensor_tensor(
+                out=kw[:].rearrange("f (u p e) -> f u p e", u=2, e=2),
+                in0=tanh_t[g, ft // 4][:, ft % 4].rearrange("f (u p e) -> f u p e", u=2, e=2),
+                in1=gain_b[:, 512 * (g - 2) : 512 * (g - 1)].rearrange("f (p u e) -> f u p e", u=2, e=2),
+                op=MULT,
+            )
+            k_wide[g, ft] = kw[:]
+
         def gains(g, ch):
-            for i in range(FPC):
-                k_gain(g, ch * FPC + i)
+            if g < 2:
+                k_gain(g, ch * FPC, FPC)
+            else:
+                for i in range(FPC):
+                    k_gain_unsorted(g, ch * FPC + i)
 
         def unit_turns(i):
             ch, half = divmod(i, 2)
@@ -453,6 +501,7 @@ def tile_networked_sliding_control_s7_kernel(tc, x_bytes, x_scale, c, offset, ga
         load_x(0, 1)
         load_b(2)
         load_x(1, 0)
+        load_gain_row()
         load_c(0, 0)
         load_c(1, 0)
         load_b(3)
@@ -474,13 +523,14 @@ def tile_networked_sliding_control_s7_kernel(tc, x_bytes, x_scale, c, offset, ga
         b_tile(2)
         load_c(1, 1)
         x_pair(0, 1)
+        sort_gain_row()
         widen_pair(1, 0)
         x_pair(1, 0)
+        spread_gain()
         b_tile(3)
         b_tile(4)
         c_inter(0, 0, "v")
         load_b(5)
-        load_gain(0)
         c_inter(1, 0, "v")
         load_b(6)
         x_quant(0)
@@ -488,7 +538,7 @@ def tile_networked_sliding_control_s7_kernel(tc, x_bytes, x_scale, c, offset, ga
         widen_pair(1, 1)
         load_xg(3)
         load_b(7)
-        load_gain(1)
+        load_gain()
         cast_pair(2, 0)
         c_inter(0, 1, "v")
         c_inter(1, 1, "v")
@@ -500,8 +550,7 @@ def tile_networked_sliding_control_s7_kernel(tc, x_bytes, x_scale, c, offset, ga
         b_tile(5)
         quant_c(1)
         x_quant(1)
-        for i in range(3):
-            k_gain(0, i, AT_XINT + 8 * KIB + KIB * i)
+        k_gain(0, 0, 3, AT_XINT + 8 * KIB)
         x_scales(2, 0)
         surfaces([(0, 4), (0, 5)])
         x_turns(2, 1)
@@ -514,15 +563,13 @@ def tile_networked_sliding_control_s7_kernel(tc, x_bytes, x_scale, c, offset, ga
         x_quant(2)
         x_sort(3, 0)
         x_sort(3, 1)
-        for i, (g, ft) in enumerate([(1, 0), (1, 1), (0, 3)]):
-            k_gain(g, ft, AT_XW + 8 * KIB + KIB * i)
+        k_gain(1, 0, 3, AT_XW + 8 * KIB)
         surfaces([(1, 4), (1, 5)])
         b_tile(6)
         x_turns(3, 0)
         x_turns(3, 1)
         x_scales(3, 0)
         x_scales(3, 1)
-        b_sort(7)
         x_quant(3)
         surfaces([(2, ft) for ft in range(4)])
         surfaces([(1, 6), (1, 7), (2, 4), (2, 5)])
@@ -532,7 +579,8 @@ def tile_networked_sliding_control_s7_kernel(tc, x_bytes, x_scale, c, offset, ga
         gains(2, 0)
         quant_b(1)
         surfaces([(3, ft) for ft in range(4)])
-        gains(1, 1)
+        k_gain(0, 3, 1)
+        k_gain(1, 3, 1)
         gains(3, 0)
         quant_b(2)
         quant_k(0)

@@ -60,10 +60,10 @@ def tile_networked_sliding_control_s7_kernel(tc, x_bytes, x_scale, c, offset, ga
 
         ring_count = {}
 
-        def ring(name, shape, dtype, slots, at, size):
+        def ring(name, shape, dtype, slots, at, size, first=0):
             i = ring_count.get(name, 0)
             ring_count[name] = i + 1
-            return pool.tile(shape, dtype, name=f"{name}{i}", align_bytes=64, offset=at + size * (i % slots))
+            return pool.tile(shape, dtype, name=f"{name}{i}", align_bytes=64, offset=at + size * ((first + i) % slots))
 
         def pass_banks(count):
             banks_taken.extend([None] * count)
@@ -365,7 +365,7 @@ def tile_networked_sliding_control_s7_kernel(tc, x_bytes, x_scale, c, offset, ga
 
         def k_copy(g, ch, eng="s"):
             if g % 2 == 0:
-                kint = ring("kint", [P, 2 * FC * 4], BF16, BUFS["kint"] // 2, AT_KINT, 4 * KIB)
+                kint = ring("kint", [P, 2 * FC * 4], BF16, BUFS["kint"] // 2, AT_KINT, 4 * KIB, 1)
                 k_int[g // 2, ch] = kint
             dst = k_int[g // 2, ch][:].bitcast(F32)[:, 512 * (g % 2) : 512 * (g % 2 + 1)]
             copy(eng, dst.rearrange("p (i f u) -> p i f u", i=FPC, u=2), k_tp[g, ch][:].rearrange("p (i u f) -> p i f u", i=FPC, u=2))
@@ -498,10 +498,10 @@ def tile_networked_sliding_control_s7_kernel(tc, x_bytes, x_scale, c, offset, ga
         load_x(0, 0)
         load_b_half(0, 1)
         load_b(1)
+        load_gain_row()
         load_x(0, 1)
         load_b(2)
         load_x(1, 0)
-        load_gain_row()
         load_c(0, 0)
         load_c(1, 0)
         load_b(3)
@@ -515,6 +515,7 @@ def tile_networked_sliding_control_s7_kernel(tc, x_bytes, x_scale, c, offset, ga
                 widen_half(0, t, q)
         b_tile(0)
         turn_offset()
+        sort_gain_row()
         b_tile(1)
         x_pair(0, 0)
         widen_pair(0, 1)
@@ -523,7 +524,6 @@ def tile_networked_sliding_control_s7_kernel(tc, x_bytes, x_scale, c, offset, ga
         b_tile(2)
         load_c(1, 1)
         x_pair(0, 1)
-        sort_gain_row()
         widen_pair(1, 0)
         x_pair(1, 0)
         spread_gain()
@@ -559,25 +559,28 @@ def tile_networked_sliding_control_s7_kernel(tc, x_bytes, x_scale, c, offset, ga
         surfaces([(0, 6), (0, 7)])
         cast_pair(3, 1)
         surfaces([(1, ft) for ft in range(4)])
-        b_sort(6)
-        x_quant(2)
         x_sort(3, 0)
+        x_quant(2)
         x_sort(3, 1)
-        k_gain(1, 0, 3, AT_XW + 8 * KIB)
+        b_sort(6)
+        k_gain(1, 0, 3, AT_KINT)
         surfaces([(1, 4), (1, 5)])
-        b_tile(6)
         x_turns(3, 0)
         x_turns(3, 1)
         x_scales(3, 0)
         x_scales(3, 1)
         x_quant(3)
         surfaces([(2, ft) for ft in range(4)])
-        surfaces([(1, 6), (1, 7), (2, 4), (2, 5)])
+        pass_banks(4)
+        surfaces([(1, 6), (1, 7)])
+        b_tile(6)
+        surfaces([(2, 4), (2, 5)])
         b_tile(7)
-        turn_unit(0)
+        unit_turns(0)
         quant_b(0)
         gains(2, 0)
         quant_b(1)
+        unit_copies(0, "v")
         surfaces([(3, ft) for ft in range(4)])
         k_gain(0, 3, 1)
         k_gain(1, 3, 1)

@@ -182,7 +182,7 @@ def tile_networked_sliding_control_s7_kernel(tc, x_bytes, x_scale, c, offset, ga
             )
 
         def cast_pair(g, u):
-            xw = ring("xc", [P, 2, K], BF16, 2, AT_XW + 4 * KIB, 4 * KIB)
+            xw = ring("xc", [P, 2, K], BF16, 3, AT_XW, 4 * KIB)
             nc.scalar.copy(out=xw[:].rearrange("p e k -> p (e k)"), in_=x_raw[g, u].rearrange("p e k -> p (e k)").bitcast(FP8))
             x_cast[g, u] = xw
             for e in range(2):
@@ -503,10 +503,10 @@ def tile_networked_sliding_control_s7_kernel(tc, x_bytes, x_scale, c, offset, ga
         load_b(2)
         load_x(1, 0)
         load_c(0, 0)
+        load_x(1, 1)
         load_c(1, 0)
         load_b(3)
         load_b(4)
-        load_x(1, 1)
         cast_offset()
         spread_scale(0, "v")
         spread_scale(1, "s")
@@ -525,9 +525,12 @@ def tile_networked_sliding_control_s7_kernel(tc, x_bytes, x_scale, c, offset, ga
         load_c(1, 1)
         x_pair(0, 1)
         widen_pair(1, 0)
-        x_pair(1, 0)
+        x_turns(1, 0)
+        cast_pair(1, 1)
+        x_copies(1, 0)
         spread_gain()
         b_tile(3)
+        x_turns(1, 1)
         b_tile(4)
         c_inter(0, 0, "v")
         load_b(5)
@@ -535,7 +538,7 @@ def tile_networked_sliding_control_s7_kernel(tc, x_bytes, x_scale, c, offset, ga
         load_b(6)
         x_quant(0)
         quant_c(0)
-        widen_pair(1, 1)
+        x_scales(1, 1)
         load_xg(3)
         load_b(7)
         load_gain()
@@ -543,7 +546,6 @@ def tile_networked_sliding_control_s7_kernel(tc, x_bytes, x_scale, c, offset, ga
         c_inter(0, 1, "v")
         c_inter(1, 1, "v")
         surfaces([(0, 0), (0, 1)])
-        x_pair(1, 1)
         cast_pair(2, 1)
         surfaces([(0, 2), (0, 3)])
         x_turns(2, 0)
@@ -576,11 +578,10 @@ def tile_networked_sliding_control_s7_kernel(tc, x_bytes, x_scale, c, offset, ga
         b_tile(6)
         surfaces([(2, 4), (2, 5)])
         b_tile(7)
-        unit_turns(0)
+        turn_unit(0)
         quant_b(0)
         gains(2, 0)
         quant_b(1)
-        unit_copies(0, "v")
         surfaces([(3, ft) for ft in range(4)])
         k_gain(0, 3, 1)
         k_gain(1, 3, 1)

@@ -316,7 +316,7 @@ def tile_networked_sliding_control_s7_kernel(tc, x_bytes, x_scale, c, offset, ga
                     out=tanh_tile(g, ft)[:, 256 * u : 256 * (u + 1)], in_=s_ps[g, u, fts][:, 256 * i : 256 * (i + 1)], func=ACT.Tanh, bias=off_cols[:, ft : ft + 1]
                 )
 
-        kw_taken = []
+        kw_taken, gain_ps = [], []
 
         def kw_place(count):
             first = len(kw_taken) % KW_SLOTS
@@ -337,7 +337,10 @@ def tile_networked_sliding_control_s7_kernel(tc, x_bytes, x_scale, c, offset, ga
             for g in range(2):
                 rows = gain_row[:, 512 * g : 512 * (g + 1)]
                 nc.tensor.matmul(out=flat[:, 512 * g : 512 * (g + 1)], lhsT=ones[:], rhs=rows, start=True, stop=True)
-            nc.scalar.copy(out=gain_s[:], in_=flat)
+            gain_ps.append(flat)
+
+        def copy_gain():
+            nc.scalar.copy(out=gain_s[:], in_=gain_ps[0])
 
         def k_gain(g, first, count, at=None):
             if at is None:
@@ -525,10 +528,11 @@ def tile_networked_sliding_control_s7_kernel(tc, x_bytes, x_scale, c, offset, ga
         load_c(1, 1)
         x_pair(0, 1)
         widen_pair(1, 0)
+        spread_gain()
         x_turns(1, 0)
         cast_pair(1, 1)
+        copy_gain()
         x_copies(1, 0)
-        spread_gain()
         b_tile(3)
         x_turns(1, 1)
         b_tile(4)
@@ -571,6 +575,7 @@ def tile_networked_sliding_control_s7_kernel(tc, x_bytes, x_scale, c, offset, ga
         x_turns(3, 1)
         x_scales(3, 0)
         x_scales(3, 1)
+        quant_b(0)
         x_quant(3)
         surfaces([(2, ft) for ft in range(4)])
         pass_banks(4)
@@ -579,25 +584,18 @@ def tile_networked_sliding_control_s7_kernel(tc, x_bytes, x_scale, c, offset, ga
         surfaces([(2, 4), (2, 5)])
         b_tile(7)
         turn_unit(0)
-        quant_b(0)
         gains(2, 0)
         quant_b(1)
         surfaces([(3, ft) for ft in range(4)])
         k_gain(0, 3, 1)
         k_gain(1, 3, 1)
         gains(3, 0)
-        quant_b(2)
         quant_k(0)
+        quant_b(2)
         quant_b(3)
         surfaces([(2, 6), (2, 7), (3, 4), (3, 5)])
-        sigma(3, 6)
-        sigma(3, 7)
-        unit_turns(1)
-        unit_turns(2)
-        unit_copies(1)
-        tanh(3, 6)
-        tanh(3, 7)
-        unit_copies(2)
+        turn_unit(1)
+        turn_unit(2)
         pairs = [(n, n + 1) for n in range(0, NT, 2)]
         for ch in range(CH - 1):
             if ch > 0:
@@ -611,6 +609,9 @@ def tile_networked_sliding_control_s7_kernel(tc, x_bytes, x_scale, c, offset, ga
             quant_k(2 * ch + 2)
             for nodes in pairs:
                 nodes_part(ch, nodes, (0, 1))
+            if ch == 0:
+                surfaces([(3, 6), (3, 7)])
+                pass_banks(6)
             for i, nodes in enumerate(pairs):
                 if ch == CH - 2 and i == 1:
                     turn_unit(2 * ch + 3)

@@ -14,6 +14,7 @@ FP8 = mybir.dt.float8_e4m3fn
 FP8X4 = mybir.dt.float8_e4m3fn_x4
 ACT = mybir.ActivationFunctionType
 MULT = mybir.AluOpType.mult
+ADD = mybir.AluOpType.add
 
 P = 128
 G = M // 512
@@ -157,12 +158,15 @@ def tile_networked_sliding_control_s7_kernel(tc, x_bytes, x_scale, c, offset, ga
         c_int, c_codes, x_codes, b_codes, k_codes = {}, {}, {}, {}, {}
         x_wide, x_tp, x_int, b_tp, b_int = {}, {}, {}, {}, {}
 
-        def c_inter(q, h, eng):
-            if q == 0:
-                cint = pool.tile([P, Q * 512 * 4], BF16, name="cint", align_bytes=64, offset=AT_CINT)
-                c_int[h] = cint
-            dst = c_int[h][:, 2048 * q : 2048 * (q + 1)].rearrange("p (c i t) -> p c t i", i=4, t=4)
-            copy(eng, dst, c_raw[q, h][:].rearrange("p t (c i) -> p c t i", i=4))
+        def c_inter(q, h, eng, first=0, last=512):
+            if q == 0 and first == 0:
+                c_int[h] = pool.tile([P, Q * 512 * 4], BF16, name=f"cint{h}", align_bytes=64, offset=AT_CINT)
+            dst = c_int[h][:, 2048 * q + 4 * first : 2048 * q + 4 * last]
+            src = c_raw[q, h][:, :, first:last]
+            if eng == "g":
+                nc.gpsimd.tensor_scalar(out=dst.rearrange("p (f t) -> p f t", t=4), in0=src.rearrange("p t f -> p f t"), scalar1=1.0, scalar2=0.0, op0=MULT, op1=ADD)
+            else:
+                copy(eng, dst.rearrange("p (c i t) -> p c t i", i=4, t=4), src.rearrange("p t (c i) -> p c t i", i=4))
 
         def quant_c(h):
             c_codes[h] = quantise(f"c{h}", c_int[h], Q * 512)
@@ -510,9 +514,9 @@ def tile_networked_sliding_control_s7_kernel(tc, x_bytes, x_scale, c, offset, ga
         load_c(1, 0)
         load_b(3)
         load_b(4)
-        cast_offset()
-        spread_scale(0, "v")
+        spread_scale(0, "s")
         spread_scale(1, "s")
+        cast_offset()
         for q in range(Q):
             for t in range(2):
                 widen_half(0, t, q)
@@ -522,9 +526,9 @@ def tile_networked_sliding_control_s7_kernel(tc, x_bytes, x_scale, c, offset, ga
         b_tile(1)
         x_pair(0, 0)
         widen_pair(0, 1)
-        load_xg(2)
         load_c(0, 1)
         b_tile(2)
+        load_xg(2)
         load_c(1, 1)
         x_pair(0, 1)
         widen_pair(1, 0)
@@ -542,12 +546,13 @@ def tile_networked_sliding_control_s7_kernel(tc, x_bytes, x_scale, c, offset, ga
         load_b(6)
         x_quant(0)
         quant_c(0)
+        c_inter(0, 1, "g", 0, 320)
         x_scales(1, 1)
         load_xg(3)
         load_b(7)
         load_gain()
         cast_pair(2, 0)
-        c_inter(0, 1, "v")
+        c_inter(0, 1, "v", 320)
         c_inter(1, 1, "v")
         surfaces([(0, 0), (0, 1)])
         cast_pair(2, 1)

from contextlib import ExitStack

import concourse.mybir as mybir
from concourse.masks import make_identity

M, K, F, N = 2048, 1024, 1024, 1024
FLOPS = 2 * M * K * F + 2 * N * M * F

F32 = mybir.dt.float32
BF16 = mybir.dt.bfloat16
U32 = mybir.dt.uint32
U8 = mybir.dt.uint8
FP8 = mybir.dt.float8_e4m3fn
FP8X4 = mybir.dt.float8_e4m3fn_x4
ACT = mybir.ActivationFunctionType
MULT = mybir.AluOpType.mult
ADD = mybir.AluOpType.add

P = 128
G = M // 512
Q = K // 512
FT = F // P
NT = N // P
CH = 4
FC = F // CH
FPC = FC // P
BANKS = 8
KW_SLOTS = 12
BUFS = {"braw": 6, "cint": 2, "xw": 6, "xint": 2, "bint": 8, "thmod": 8, "kw": 12, "kint": 6, "xb": 4, "vo": 12}
KIB = 1024
AT_RAW = 0
AT_KW, AT_KINT = AT_RAW, AT_RAW + 12 * KIB
AT_XB = AT_RAW + 24 * KIB
AT_XW = AT_XB + 8 * KIB
AT_VO = AT_XW
AT_XINT = AT_XW + 12 * KIB
AT_BINT = AT_XINT + 16 * KIB
AT_TH = AT_BINT + 32 * KIB
AT_CINT = AT_TH + 56 * KIB
AT_SORT = AT_TH + 40 * KIB


def tile_networked_sliding_control_s7_kernel(tc, x_bytes, x_scale, c, offset, gain, bmat, out):
    nc = tc.nc
    with ExitStack() as ctx:
        const = ctx.enter_context(tc.tile_pool(name="const", bufs=1))
        kept = ctx.enter_context(tc.tile_pool(name="kept", bufs=1))
        pool = ctx.enter_context(tc.tile_pool(name="work", bufs=1))
        psum = ctx.enter_context(tc.psum_pool(name="psum", bufs=1))

        x_view = x_bytes.rearrange("(g p u e) k -> g u p e k", p=P, u=2, e=2)
        c_view = c.rearrange("(q p j) (h f) -> q h p j f", p=P, j=4, h=2)
        b_view = bmat.rearrange("(n p) m -> n p m", p=P)
        x_raw, c_raw, b_raw, b_whole, b_sorted, x_sorted, x_cast = {}, {}, {}, {}, {}, {}, {}
        banks_taken, kept_widths = [], []

        def bank():
            tile = psum.tile([P, 512], F32, name=f"bank{len(banks_taken) % BANKS}")
            banks_taken.append(tile)
            return tile

        ring_count = {}

        def ring(name, shape, dtype, slots, at, size, first=0):
            i = ring_count.get(name, 0)
            ring_count[name] = i + 1
            return pool.tile(shape, dtype, name=f"{name}{i}", align_bytes=64, offset=at + size * ((first + i) % slots))

        def pass_banks(count):
            banks_taken.extend([None] * count)

        def copy(eng, dst, src):
            if eng == "v":
                nc.vector.tensor_copy(out=dst, in_=src)
            else:
                nc.scalar.copy(out=dst, in_=src)

        def code_tiles(name, width):
            first = 5 * sum(kept_widths)
            kept_widths.append(width)
            codes = kept.tile([P, width], U32, name=f"codes_{name}", align_bytes=256, offset=first)
            scales = kept.tile([P, width], U8, name=f"scales_{name}", align_bytes=256, offset=first + 4 * width)
            return codes, scales

        def quantise_into(tiles, src, first, width):
            codes, scales = tiles
            words = slice(first, first + width)
            nc.vector.quantize_mx(out=codes[:, words].bitcast(FP8X4), scales=scales[:, words], in_=src[:, 4 * first : 4 * (first + width)])

        def quantise(name, src, width):
            tiles = code_tiles(name, width)
            quantise_into(tiles, src, 0, width)
            return tiles

        def load_x(g, u):
            xbytes = ring("xbytes", [P, 2, K], U8, BUFS["xb"], AT_XB, 2 * KIB)
            nc.sync.dma_start(out=xbytes[:], in_=x_view[g, u])
            x_raw[g, u] = xbytes[:]

        def load_xg(g):
            xgroup = pool.tile([P, 2, 2, K], U8, name=f"xbytes_group{g}", align_bytes=64, offset=AT_XB + 4 * KIB * (g % 2))
            nc.sync.dma_start(out=xgroup[:].rearrange("p u e k -> p (u e k)"), in_=x_bytes.rearrange("(g p t) k -> g p (t k)", p=P, t=4)[g])
            for u in range(2):
                x_raw[g, u] = xgroup[:, u]

        def load_c(q, h):
            raw = ring("raw", [P, 4, 512], BF16, BUFS["braw"], AT_RAW, 4 * KIB)
            nc.sync.dma_start(out=raw[:], in_=c_view[q, h])
            c_raw[q, h] = raw

        def load_b(n):
            raw = ring("raw", [P, M], BF16, BUFS["braw"], AT_RAW, 4 * KIB)
            nc.sync.dma_start(out=raw[:], in_=b_view[n])
            b_raw[n] = [raw[:, 0 : M // 2], raw[:, M // 2 : M]]
            b_whole[n] = raw

        def load_b_half(n, half):
            raw = pool.tile([P, M // 2], BF16, name=f"raw_half{half}", align_bytes=64, offset=AT_TH + 2 * KIB * half)
            nc.sync.dma_start(out=raw[:], in_=b_view[n][:, half * M // 2 : (half + 1) * M // 2])
            b_raw.setdefault(n, []).append(raw[:])

        ident = const.tile([P, P], F32)
        off_rows = const.tile([P, P], BF16)
        scale_b = const.tile([P, K], F32)
        gain_b = const.tile([P, M // 2], BF16)
        ones = const.tile([P, P], BF16)
        gain_raw = pool.tile([1, M // 2], BF16, name="gain_raw", align_bytes=64, offset=AT_TH + 12 * KIB)
        gain_row = pool.tile([P, M // 2], BF16, name="gain_row", align_bytes=64, offset=AT_TH + 8 * KIB)
        gain_s = const.tile([P, M // 2], BF16)
        scale_v = const.tile([P, Q, 4], F32)
        off_f = const.tile([P, P], F32)
        off_cols = const.tile([P, FT], F32)

        def load_scale():
            nc.scalar.dma_start(out=scale_v[:], in_=x_scale.rearrange("o (q p m) -> p (o q) m", p=P, m=4))

        def load_offset():
            nc.scalar.dma_start(out=off_rows[0:FT, :], in_=offset.rearrange("(c p) -> c p", p=P))

        def load_gain():
            nc.sync.dma_start(out=gain_b[:], in_=gain[M // 2 : M].partition_broadcast(P))

        def spread_scale(q, eng):
            sp = bank()
            for m in range(4):
                nc.tensor.transpose(sp[:, m * P : (m + 1) * P], scale_v[:, q, m : m + 1].to_broadcast([P, P]), ident[:])
            dst = scale_b[:, 512 * q : 512 * (q + 1)].rearrange("p (n m) -> p n m", m=4)
            copy(eng, dst, sp[:].rearrange("p (m n) -> p n m", m=4))

        def cast_offset():
            nc.scalar.copy(out=off_f[:], in_=off_rows[:])

        def turn_offset():
            off_ps = bank()
            nc.tensor.transpose(off_ps[:, 0:P], off_f[:], ident[:])
            nc.scalar.copy(out=off_cols[:], in_=off_ps[:, 0:FT])

        c_int, c_codes, x_codes, b_codes, k_codes = {}, {}, {}, {}, {}
        x_wide, x_tp, x_int, b_tp, b_int = {}, {}, {}, {}, {}

        def c_inter(q, h, eng, first=0, last=512):
            if q == 0 and first == 0:
                c_int[h] = pool.tile([P, Q * 512 * 4], BF16, name=f"cint{h}", align_bytes=64, offset=AT_CINT)
            dst = c_int[h][:, 2048 * q + 4 * first : 2048 * q + 4 * last]
            src = c_raw[q, h][:, :, first:last]
            if eng == "g":
                nc.gpsimd.tensor_scalar(out=dst.rearrange("p (f t) -> p f t", t=4), in0=src.rearrange("p t f -> p f t"), scalar1=1.0, scalar2=0.0, op0=MULT, op1=ADD)
            else:
                copy(eng, dst.rearrange("p (c i t) -> p c t i", i=4, t=4), src.rearrange("p t (c i) -> p c t i", i=4))

        def quant_c(h):
            c_codes[h] = quantise(f"c{h}", c_int[h], Q * 512)

        def widen(g, t):
            xw = ring("xw", [P, K], BF16, BUFS["xw"], AT_XW, 2 * KIB)
            nc.vector.tensor_tensor(out=xw[:], in0=x_raw[g, t // 2][:, t % 2, :].bitcast(FP8), in1=scale_b[:], op=MULT)
            x_wide[g, t] = xw

        def widen_half(g, t, q):
            if q == 0:
                xw = ring("xw", [P, K], BF16, BUFS["xw"], AT_XW, 2 * KIB)
                x_wide[g, t] = xw
            states = slice(512 * q, 512 * (q + 1))
            nc.vector.tensor_tensor(
                out=x_wide[g, t][:, states], in0=x_raw[g, t // 2][:, t % 2, states].bitcast(FP8), in1=scale_b[:, states], op=MULT
            )

        def cast_pair(g, u):
            xw = ring("xc", [P, 2, K], BF16, 3, AT_XW, 4 * KIB)
            nc.scalar.copy(out=xw[:].rearrange("p e k -> p (e k)"), in_=x_raw[g, u].rearrange("p e k -> p (e k)").bitcast(FP8))
            x_cast[g, u] = xw
            for e in range(2):
                x_wide[g, 2 * u + e] = xw[:, e]

        def x_scale_out(g, u, q):
            if (u, q) == (0, 0):
                x_int[g] = pool.tile([P, Q * 512 * 4], BF16, name=f"xscaled{g}", align_bytes=64, offset=(AT_XINT, AT_CINT)[g % 2])
            first = 2048 * q + 1024 * u
            nc.vector.tensor_tensor(
                out=x_int[g][:, first : first + 1024].rearrange("p (r e w h) -> p r e w h", e=2, w=2, h=2),
                in0=x_tp[g, u, q][:].bitcast(BF16).rearrange("p (e w r h) -> p r e w h", e=2, w=2, h=2),
                in1=scale_v[:, q].rearrange("p (r e w h) -> p r e w h", r=1, e=1, h=2).to_broadcast([P, P, 2, 2, 2]),
                op=MULT,
            )

        def sort_words(dst, src):
            nc.vector.tensor_copy(out=dst.rearrange("p (g w r) -> p g w r", w=2, r=P), in_=src.rearrange("p (g r w) -> p g w r", w=2, r=P))

        def b_sort(n):
            b_sorted[n] = ring("sorted", [P, M // 2], F32, 3, AT_SORT, 4 * KIB)
            sort_words(b_sorted[n][:], b_whole[n][:].bitcast(F32))

        def x_sort(g, u):
            x_sorted[g, u] = ring("sorted", [P, K], F32, 3, AT_SORT, 4 * KIB)
            sort_words(x_sorted[g, u][:], x_cast[g, u][:].rearrange("p e k -> p (e k)").bitcast(F32))

        def x_turn(g, u, q):
            tp = bank()
            for e in range(2):
                for w in range(2):
                    i = 2 * e + w
                    if (g, u) in x_sorted:
                        words = x_sorted[g, u][:, 512 * e + 256 * q + P * w : 512 * e + 256 * q + P * (w + 1)]
                    else:
                        words = x_wide[g, 2 * u + e][:].bitcast(F32)[:, 256 * q + w : 256 * (q + 1) : 2]
                    nc.tensor.transpose(tp[:, i * P : (i + 1) * P], words, ident[:])
            x_tp[g, u, q] = tp

        def x_copy(g, u, q, eng="s"):
            if (u, q) == (0, 0):
                xint = ring("xint", [P, Q * 512 * 4], BF16, BUFS["xint"], AT_XINT, 8 * KIB)
                x_int[g] = xint
            first = 1024 * q + 512 * u
            dst = x_int[g][:].bitcast(F32)[:, first : first + 512]
            copy(eng, dst.rearrange("p (r i) -> p r i", i=4), x_tp[g, u, q][:].rearrange("p (i r) -> p r i", i=4))

        def x_quant(g):
            x_codes[g] = quantise(f"x{g}", x_int[g], Q * 512)

        def x_quant_pair(g, u):
            if u == 0:
                x_codes[g] = code_tiles(f"x{g}", Q * 512)
            for q in range(Q):
                quantise_into(x_codes[g], x_int[g], 512 * q + 256 * u, 256)

        def b_turn(n, half):
            tp = bank()
            for gl in range(2):
                for w in range(2):
                    i = 2 * gl + w
                    if n in b_sorted:
                        words = b_sorted[n][:, 512 * half + P * i : 512 * half + P * (i + 1)]
                    else:
                        words = b_raw[n][half].bitcast(F32)[:, 256 * gl + w : 256 * (gl + 1) : 2]
                    nc.tensor.transpose(tp[:, i * P : (i + 1) * P], words, ident[:])
            b_tp[n, half] = tp

        def b_copy(n, half, eng="s"):
            if n % 2 == 0 and half == 0:
                bint = ring("bint", [P, 2 * G * P * 4], BF16, NT // 2, AT_BINT, 8 * KIB)
                b_int[n // 2] = bint
            first = 1024 * (n % 2) + 512 * half
            dst = b_int[n // 2][:].bitcast(F32)[:, first : first + 512]
            copy(eng, dst.rearrange("p (g r w) -> p g r w", g=2, w=2), b_tp[n, half][:].rearrange("p (g w r) -> p g r w", g=2, w=2))

        def quant_b(pair):
            b_codes[pair] = quantise(f"b{pair}", b_int[pair], 2 * G * P)

        s_ps, tanh_t, k_wide, k_tp, k_int, v_ps = {}, {}, {}, {}, {}, {}

        def sigma(g, ft):
            ps = bank()
            xc, xs = x_codes[g]
            cc, cs = c_codes[ft // 4]
            for q in range(Q):
                col = slice(512 * q + (ft % 4) * P, 512 * q + (ft % 4 + 1) * P)
                agents = slice(512 * q, 512 * (q + 1))
                nc.tensor.matmul_mx(
                    out=ps[:],
                    lhsT=cc[:, col].bitcast(FP8X4),
                    lhsT_scale=cs[:, col],
                    rhs=xc[:, agents].bitcast(FP8X4),
                    rhs_scale=xs[:, agents],
                    start=(q == 0),
                    stop=(q == Q - 1),
                )
            s_ps[g, ft] = ps

        def tanh_tile(g, ft):
            h, i = divmod(ft, 4)
            if (g, h) not in tanh_t:
                tanh_t[g, h] = pool.tile([P, 4, 512], F32, name=f"th{g}{h}", align_bytes=64, offset=AT_TH + 8 * KIB * len(tanh_t))
            return tanh_t[g, h][:, i]

        def tanh(g, ft):
            nc.scalar.activation(out=tanh_tile(g, ft), in_=s_ps[g, ft][:], func=ACT.Tanh, bias=off_cols[:, ft : ft + 1])

        def sigma_pair(g, u, fts):
            ps = bank()
            xc, xs = x_codes[g]
            for i, ft in enumerate(fts):
                cc, cs = c_codes[ft // 4]
                for q in range(Q):
                    col = slice(512 * q + (ft % 4) * P, 512 * q + (ft % 4 + 1) * P)
                    agents = slice(512 * q + 256 * u, 512 * q + 256 * (u + 1))
                    nc.tensor.matmul_mx(
                        out=ps[:, 256 * i : 256 * (i + 1)],
                        lhsT=cc[:, col].bitcast(FP8X4),
                        lhsT_scale=cs[:, col],
                        rhs=xc[:, agents].bitcast(FP8X4),
                        rhs_scale=xs[:, agents],
                        start=(q == 0),
                        stop=(q == Q - 1),
                    )
            s_ps[g, u, fts] = ps

        def tanh_pair(g, u, fts):
            for i, ft in enumerate(fts):
                nc.scalar.activation(
                    out=tanh_tile(g, ft)[:, 256 * u : 256 * (u + 1)], in_=s_ps[g, u, fts][:, 256 * i : 256 * (i + 1)], func=ACT.Tanh, bias=off_cols[:, ft : ft + 1]
                )

        kw_taken, gain_ps = [], []

        def kw_place(count):
            first = len(kw_taken) % KW_SLOTS
            kw_taken.extend([None] * count)
            return AT_KW + KIB * first

        def load_gain_row():
            nc.sync.dma_start(out=gain_raw[:], in_=gain[0 : M // 2].rearrange("(o m) -> o m", o=1))

        def sort_gain_row():
            nc.scalar.copy(
                out=gain_row[0:1, :].bitcast(F32).rearrange("p (g w r) -> p g w r", w=2, r=P),
                in_=gain_raw[:].bitcast(F32).rearrange("p (g r w) -> p g w r", w=2, r=P),
            )

        def spread_gain():
            flat = bank()[:].bitcast(BF16)
            for g in range(2):
                rows = gain_row[:, 512 * g : 512 * (g + 1)]
                nc.tensor.matmul(out=flat[:, 512 * g : 512 * (g + 1)], lhsT=ones[:], rhs=rows, start=True, stop=True)
            gain_ps.append(flat)

        def copy_gain():
            nc.scalar.copy(out=gain_s[:], in_=gain_ps[0])

        def k_gain(g, first, count, at=None):
            if at is None:
                kw = pool.tile([P, count, 512], BF16, name=f"kw{g}{first}", align_bytes=64, offset=kw_place(count))
            else:
                kw = pool.tile([P, count, 512], BF16, name=f"kw_pool{g}", align_bytes=64, offset=at)
            h, i = divmod(first, 4)
            (nc.vector if at is None else nc.gpsimd).tensor_tensor(
                out=kw[:],
                in0=tanh_t[g, h][:, i : i + count],
                in1=gain_s[:, 512 * g : 512 * (g + 1)].rearrange("f (o a) -> f o a", o=1).to_broadcast([P, count, 512]),
                op=MULT,
            )
            for j in range(count):
                k_wide[g, first + j] = kw[:, j]

        def k_turn(g, ch):
            tp = bank()
            for i in range(FPC):
                words = k_wide[g, ch * FPC + i].bitcast(F32)
                for u in range(2):
                    j = 2 * i + u
                    nc.tensor.transpose(tp[:, j * P : (j + 1) * P], words[:, P * u : P * (u + 1)], ident[:])
            k_tp[g, ch] = tp

        def k_copy(g, ch, eng="s"):
            if g % 2 == 0:
                kint = ring("kint", [P, 2 * FC * 4], BF16, BUFS["kint"] // 2, AT_KINT, 4 * KIB, 1)
                k_int[g // 2, ch] = kint
            dst = k_int[g // 2, ch][:].bitcast(F32)[:, 512 * (g % 2) : 512 * (g % 2 + 1)]
            copy(eng, dst.rearrange("p (i f u) -> p i f u", i=FPC, u=2), k_tp[g, ch][:].rearrange("p (i u f) -> p i f u", i=FPC, u=2))

        def quant_k(unit):
            ch, half = divmod(unit, 2)
            k_codes[half, ch] = quantise(f"k{unit}", k_int[half, ch], 2 * FC)

        def nodes_part(ch, nodes, groups, first=0, width=FC):
            if groups[0] == 0:
                v_ps[ch, nodes, first] = bank()
            ps = v_ps[ch, nodes, first]
            for g in groups:
                kc, ks = k_codes[g // 2, ch]
                cols = slice(FC * (g % 2) + first, FC * (g % 2) + first + width)
                for i, n in enumerate(nodes):
                    bc, bs = b_codes[n // 2]
                    rows = slice(512 * (n % 2) + P * g, 512 * (n % 2) + P * (g + 1))
                    nc.tensor.matmul_mx(
                        out=ps[:, width * i : width * (i + 1)],
                        lhsT=bc[:, rows].bitcast(FP8X4),
                        lhsT_scale=bs[:, rows],
                        rhs=kc[:, cols].bitcast(FP8X4),
                        rhs_scale=ks[:, cols],
                        start=(g == 0 and i == 0),
                        stop=(g == G - 1 and i == len(nodes) - 1),
                    )

        def store_nodes(ch, nodes, eng="s", first=0, width=FC):
            vo = ring("vo", [P, 2 * FC], F32, BUFS["vo"], AT_VO, 2 * KIB)
            used = width * len(nodes)
            copy(eng, vo[:, 0:used], v_ps[ch, nodes, first][:, 0:used])
            rows = slice(nodes[0] * P, (nodes[-1] + 1) * P)
            cols = slice(ch * FC + first, ch * FC + first + width)
            nc.sync.dma_start(
                out=out[rows, cols].rearrange("(i p) f -> p i f", p=P),
                in_=vo[:, 0:used].rearrange("p (i f) -> p i f", f=width),
            )

        ctx.enter_context(tc.manual_schedule())
        nc.vector.memset(ident[:], 0.0)
        make_identity(nc, ident[:], nomemset=True)
        nc.vector.memset(off_rows[:], 0.0)
        nc.vector.memset(ones[:], 1.0)
        nc.gpsimd.memset(gain_row[:].bitcast(U32), 0)
        def x_turns(g, u):
            for q in range(Q):
                x_turn(g, u, q)

        def x_copies(g, u, eng="s"):
            for q in range(Q):
                x_copy(g, u, q, eng)

        def x_scales(g, u):
            for q in range(Q):
                x_scale_out(g, u, q)

        def x_pair(g, u):
            x_turns(g, u)
            x_copies(g, u)

        def b_turns(n):
            for half in range(2):
                b_turn(n, half)

        def b_copies(n, eng="s"):
            for half in range(2):
                b_copy(n, half, eng)

        def b_tile(n):
            b_turns(n)
            b_copies(n)

        def surfaces(tiles):
            for g, ft in tiles:
                sigma(g, ft)
            for g, ft in tiles:
                tanh(g, ft)

        def surfaces_pair(g, u, h):
            halves = [(4 * h, 4 * h + 1), (4 * h + 2, 4 * h + 3)]
            for fts in halves:
                sigma_pair(g, u, fts)
            for fts in halves:
                tanh_pair(g, u, fts)

        def widen_pair(g, u):
            widen(g, 2 * u)
            widen(g, 2 * u + 1)

        def k_gain_unsorted(g, ft):
            kw = pool.tile([P, 512], BF16, name=f"kw{g}{ft}", align_bytes=64, offset=kw_place(1))
            nc.vector.tensor_tensor(
                out=kw[:].rearrange("f (u p e) -> f u p e", u=2, e=2),
                in0=tanh_t[g, ft // 4][:, ft % 4].rearrange("f (u p e) -> f u p e", u=2, e=2),
                in1=gain_b[:, 512 * (g - 2) : 512 * (g - 1)].rearrange("f (p u e) -> f u p e", u=2, e=2),
                op=MULT,
            )
            k_wide[g, ft] = kw[:]

        def gains(g, ch):
            if g < 2:
                k_gain(g, ch * FPC, FPC)
            else:
                for i in range(FPC):
                    k_gain_unsorted(g, ch * FPC + i)

        def unit_turns(i):
            ch, half = divmod(i, 2)
            for g in (2 * half, 2 * half + 1):
                k_turn(g, ch)

        def unit_copies(i, eng="s"):
            ch, half = divmod(i, 2)
            for g in (2 * half, 2 * half + 1):
                k_copy(g, ch, eng)

        def turn_unit(i):
            unit_turns(i)
            unit_copies(i)

        def gain_unit(i):
            ch, half = divmod(i, 2)
            gains(2 * half, ch)
            gains(2 * half + 1, ch)

        load_scale()
        load_offset()
        load_b_half(0, 0)
        load_x(0, 0)
        load_b_half(0, 1)
        load_b(1)
        load_gain_row()
        load_x(0, 1)
        load_b(2)
        load_x(1, 0)
        load_c(0, 0)
        load_x(1, 1)
        load_c(1, 0)
        load_b(3)
        load_b(4)
        spread_scale(0, "s")
        spread_scale(1, "s")
        cast_offset()
        for q in range(Q):
            for t in range(2):
                widen_half(0, t, q)
        b_tile(0)
        turn_offset()
        sort_gain_row()
        b_tile(1)
        x_pair(0, 0)
        widen_pair(0, 1)
        load_c(0, 1)
        b_tile(2)
        load_xg(2)
        load_c(1, 1)
        x_pair(0, 1)
        widen_pair(1, 0)
        spread_gain()
        x_turns(1, 0)
        cast_pair(1, 1)
        copy_gain()
        x_copies(1, 0)
        b_tile(3)
        x_turns(1, 1)
        b_tile(4)
        c_inter(0, 0, "v")
        load_b(5)
        c_inter(1, 0, "v")
        load_b(6)
        x_quant(0)
        quant_c(0)
        c_inter(0, 1, "g", 0, 320)
        x_scales(1, 1)
        load_xg(3)
        load_b(7)
        load_gain()
        cast_pair(2, 0)
        c_inter(0, 1, "v", 320)
        c_inter(1, 1, "v")
        surfaces([(0, 0), (0, 1)])
        cast_pair(2, 1)
        surfaces([(0, 2), (0, 3)])
        x_turns(2, 0)
        b_tile(5)
        quant_c(1)
        x_quant(1)
        k_gain(0, 0, 3, AT_XINT + 8 * KIB)
        x_scales(2, 0)
        surfaces([(0, 4), (0, 5)])
        x_turns(2, 1)
        cast_pair(3, 0)
        x_scales(2, 1)
        surfaces([(0, 6), (0, 7)])
        cast_pair(3, 1)
        surfaces([(1, ft) for ft in range(4)])
        x_sort(3, 0)
        x_quant(2)
        x_sort(3, 1)
        b_sort(6)
        k_gain(1, 0, 3, AT_KINT)
        surfaces([(1, 4), (1, 5)])
        x_turns(3, 0)
        x_turns(3, 1)
        x_scales(3, 0)
        x_scales(3, 1)
        quant_b(0)
        x_quant(3)
        surfaces([(2, ft) for ft in range(4)])
        pass_banks(4)
        surfaces([(1, 6), (1, 7)])
        b_tile(6)
        surfaces([(2, 4), (2, 5)])
        b_tile(7)
        turn_unit(0)
        gains(2, 0)
        quant_b(1)
        surfaces([(3, ft) for ft in range(4)])
        k_gain(0, 3, 1)
        k_gain(1, 3, 1)
        gains(3, 0)
        quant_k(0)
        quant_b(2)
        quant_b(3)
        surfaces([(2, 6), (2, 7), (3, 4), (3, 5)])
        turn_unit(1)
        turn_unit(2)
        pairs = [(n, n + 1) for n in range(0, NT, 2)]
        for ch in range(CH - 1):
            if ch > 0:
                turn_unit(2 * ch + 1)
                turn_unit(2 * ch + 2)
            gains(2, ch + 1)
            quant_k(2 * ch + 1)
            gains(3, ch + 1)
            if ch + 2 < CH:
                gain_unit(2 * ch + 4)
            quant_k(2 * ch + 2)
            for nodes in pairs:
                nodes_part(ch, nodes, (0, 1))
            if ch == 0:
                surfaces([(3, 6), (3, 7)])
                pass_banks(6)
            for i, nodes in enumerate(pairs):
                if ch == CH - 2 and i == 1:
                    turn_unit(2 * ch + 3)
                    quant_k(2 * ch + 3)
                nodes_part(ch, nodes, (2, 3))
                store_nodes(ch, nodes)
        for nodes in pairs[:2]:
            nodes_part(CH - 1, nodes, (0, 1))
        for i, nodes in enumerate(pairs[:2] + [(n,) for n in range(NT - 4, NT)]):
            nodes_part(CH - 1, nodes, (2, 3) if i < 2 else (0, 1, 2, 3))
            store_nodes(CH - 1, nodes, "v" if i % 2 else "s")
